import numpy as np, ml_dtypes
CORES = [16,18,20,22]
N = 4
import mx_ref
BF = ml_dtypes.bfloat16
def entries(a):
    return np.ascontiguousarray(a.T).reshape(-1)
def table(e):
    return np.ascontiguousarray(np.reshape(e, (-1, 16)).T).astype(np.int32)
def cols(t, e):
    v = np.concatenate([t.reshape(128, -1, 4), np.zeros((128, 1, 4), BF)], axis=1)
    return np.ascontiguousarray(v[:, e]).reshape(128, -1)
def cut(t, i, w=512):
    return t[:, w * i:w * i + w]
def f(rng, *shape):
    return mx_ref.flush((rng.standard_normal(shape, dtype=np.float32) * np.exp2(rng.integers(-2, 3, shape[:-1] + (1,)))).astype(BF))
def wide(rng, *shape, cols=0):
    v = rng.standard_normal(shape, dtype=np.float32) * np.exp2(rng.integers(-12, 13, shape)).astype(np.float32)
    if cols: v *= np.repeat(np.exp2(rng.integers(-cols, cols + 1, shape[:-2] + (1, shape[-1] // 4))) * (rng.random(shape[:-2] + (1, shape[-1] // 4)) > 0.0625), 4, axis=-1).astype(np.float32)
    return mx_ref.flush(v.astype(BF))
T, CAPP, F = 128, 160, 8
def inverse(e):
    o = np.full(F * T, -1)
    k = np.flatnonzero(e >= 0); k = k[np.argsort(e[k], kind="stable")]; v = e[k]
    at = np.arange(len(k)) - np.searchsorted(v, v); keep = at < F
    o[(F * v + at)[keep]] = k[keep]
    return o
def counts(rng, most=CAPP):
    n = np.zeros((N, N), int)
    for r in range(N):
        a = rng.integers(T // N, 4 * T // N + 1, N)
        n[:, r] = a + np.bincount(rng.permutation(np.repeat(np.arange(N), most - a))[:4 * T - a.sum()], minlength=N)
    return n
def senders(rng, n):
    return np.stack([rng.permutation(np.repeat(np.arange(N), n[:, r])) for r in range(N)])
def lists(rng, A, node=None, top=None, popular=False, big=None):
    sn = np.full((N, N * CAPP), -1); nb = np.zeros((N, 4 * T), int)
    for s in range(N):
        d, e = np.nonzero(A == s); free = rng.permutation(T)
        if node is not None: v = node[d, e]
        elif top is not None:
            t = top[d, e]; h = (t.sum() + F - 1) // F; v = np.zeros(len(d), int); big.append(free[:h])
            v[t] = rng.permutation(np.repeat(free[:h], F))[:t.sum()]
            v[~t] = rng.permutation(np.repeat(free[h:], F))[:(~t).sum()]
        else:
            h = len(d) // 16 if popular else 0
            v = rng.permutation(np.concatenate([np.repeat(free[:h], F), rng.permutation(np.repeat(free[h:], F))[:len(d) - F * h]]))
        for q in range(N):
            k = np.flatnonzero(d == q); c = rng.permutation(CAPP)[:len(k)]
            sn[s, q * CAPP + c] = v[k]; nb[q, e[k]] = s * CAPP + c
    return {"sn": np.stack([table(a) for a in sn]), "nb": np.stack([table(a) for a in nb]), "il": np.stack([table(inverse(a)) for a in sn])}
def setup_inputs(rng):
    return {"x": f(rng, N, 128, 4 * T), "gr": f(rng, N, 128, 4 * T), "w": np.repeat(f(rng, 1, 128, 2048), N, axis=0), "w2": np.repeat(f(rng, 1, 128, 2048), N, axis=0), **lists(rng, senders(rng, counts(rng)))}
def setup_inputs_ties(rng):
    d = setup_inputs(rng); own = d["x"].reshape(N, 128, T, 4)
    d["x"] = np.ascontiguousarray(np.where(rng.random((N, 1, T, 1)) < 0.7, own[:1], own)).reshape(N, 128, 4 * T)
    n = counts(rng, min(CAPP, T)); A = np.zeros((N, 4 * T), int); node = np.zeros((N, 4 * T), int)
    e = np.arange(4 * T); j = e % T; k = (e // T + j) % 4
    for r in range(N):
        o = rng.permutation(N); to = 4 * rng.permutation(T)[j] + k
        A[r, to] = np.repeat(o, n[o, r]); node[r, to] = rng.permutation(T)[j]
    return {**d, **lists(rng, A, node=node)}
def setup_inputs_oneside(rng):
    d = setup_inputs(rng); top = np.zeros((N, 4 * T), bool); big = []
    for r in range(N): top[r, 4 * rng.permutation(T)[:T // 2] + 3] = True
    d.update(lists(rng, senders(rng, counts(rng)), top=top, big=big))
    v = np.abs(d["x"].astype(np.float32)).reshape(N, 128, T, 4)
    for s in range(N): v[s][:, big[s]] *= 64
    d["x"] = v.reshape(N, 128, 4 * T).astype(BF); d["w"] = np.abs(d["w"].astype(np.float32)).astype(BF)
    return d
def setup_inputs_popular(rng):
    return {**setup_inputs(rng), **lists(rng, senders(rng, counts(rng)), popular=True)}
def setup_inputs_full(rng):
    n = np.zeros((N, N), int); o = rng.permutation(N); at = rng.permutation(N)
    m = 4 * T // CAPP; rest = 4 * T - m * CAPP
    for r in range(N):
        for j in range(m): n[o[(at[r] + j) % N], r] = CAPP
        if rest: n[o[(at[r] + m) % N], r] = rest
    return {**setup_inputs(rng), **lists(rng, senders(rng, n))}
def setup_inputs_spread(rng):
    d = setup_inputs(rng); d["x"] = wide(rng, N, 128, 4 * T, cols=8); return d
def check_inputs(d):
    b = []
    for t in ("w", "w2"):
        if (d[t] != d[t][:1]).any(): b.append(t)
    e = np.stack([entries(a) for a in d["sn"]])
    if e.min() < -1 or e.max() >= T: b.append("sn")
    e = np.clip(e, -1, T - 1)
    for r in range(N):
        if np.bincount(e[r][e[r] >= 0], minlength=T).max() > F: b.append("sn")
        if not np.array_equal(np.sort(entries(d["nb"][r])), np.flatnonzero(e[:, r * CAPP:(r + 1) * CAPP].reshape(-1) >= 0)): b.append("nb")
        if not np.array_equal(entries(d["il"][r]), inverse(e[r])): b.append("il")
    return b
def four(v):
    return [mx_ref.quantize(np.ascontiguousarray(cut(v, b))) for b in range(4)]
def reference(x, gr, w, w2, sn, nb, il):
    G = []
    for r in range(N):
        arrived = mx_ref.quantize(np.concatenate([cols(x[s], entries(sn[s])[r * CAPP:(r + 1) * CAPP]) for s in range(N)], axis=1))
        e = entries(nb[r])
        z = [mx_ref.matmul(W, arrived)[:, e].reshape(128, T, 4) + np.float32(0.0) for W in four(w[r])]
        win = np.stack([v.argmax(axis=2) for v in z], axis=2)
        g = gr[r].reshape(128, T, 4); back = np.zeros((128, N * CAPP, 4), BF)
        for k in range(4): back[:, e[k::4]] = np.where(win == k, g, np.zeros_like(g))
        G.append(back)
    y = np.zeros((N, 128, 4 * T), np.float32)
    for s in range(N):
        q = mx_ref.quantize(np.concatenate([G[r][:, s * CAPP:(s + 1) * CAPP].reshape(128, -1) for r in range(N)], axis=1))
        e = entries(il[s])
        for b, V in enumerate(four(w2[s])):
            u = mx_ref.matmul(V, q); t = np.zeros((128, T), np.float32)
            for i in range(F):
                k = e[i::F]; has = k >= 0
                t[:, has] += u[:, k[has]]
            y[s][:, T * b:T * b + T] = t
    return {"y": y}

@@ -1,0 +1,391 @@
+import numpy as np
+from concourse.bass import DstId, RemoteDMATransfer
+from concourse.mybir import dt, AluOpType, ActivationFunctionType
+
+N, NODES, CAP, F = 4, 128, 160, 8
+SL = N * CAP
+RM = SL - CAP
+UW = SL + 8
+ORDER = (0, 2, 1, 3)
+
+SCRATCH = {
+    "snl": ("sbuf", [128, SL // 16], "int32"),
+    "nbl": ("sbuf", [128, 32], "int32"), "nb1": ("sbuf", [128, 32], "int32"), "nb2": ("sbuf", [128, 32], "int32"),
+    "nbo": ("sbuf", [128, 32], "uint16"), "dnb": ("dram", [16, 32], "int32"),
+    "ill": ("sbuf", [128, 64], "int32"), "il1": ("sbuf", [128, 64], "int32"), "il2": ("sbuf", [128, 64], "int32"),
+    "il3": ("sbuf", [128, 64], "int32"), "il4": ("sbuf", [128, 64], "int32"),
+    "ilo": ("sbuf", [128, 64], "uint16"), "dil": ("dram", [16, 64], "int32"),
+    "pidx": ("sbuf", [128, 1], "int32"), "p12": ("sbuf", [128, 1], "int32"), "p3": ("sbuf", [128, 1], "int32"),
+    "p15": ("sbuf", [128, 1], "int32"), "p12f": ("sbuf", [128, 1], "float32"), "p15f": ("sbuf", [128, 1], "float32"),
+    "ppf": ("sbuf", [128, 1], "float32"), "gio": ("sbuf", [128, 32], "int32"), "glo": ("sbuf", [128, 32], "uint16"),
+    "tm": ("sbuf", [128, SL], "bfloat16"), "m16": ("sbuf", [128, SL], "bfloat16"), "rr": ("sbuf", [128, SL], "bfloat16"),
+    "vals": ("sbuf", [128, 512], "float32"), "inv": ("sbuf", [128, SL], "float32"),
+    "sc1": ("sbuf", [128, SL], "float32"), "sc2": ("sbuf", [128, SL], "float32"),
+    "iv": ("sbuf", [128, 40], "int32"), "ivh": ("sbuf", [128, 40], "int32"),
+    "lt1": ("sbuf", [128, 40], "uint16"), "lt2": ("sbuf", [128, 40], "uint16"),
+    "xt": ("sbuf", [128, 512], "bfloat16"), "grt": ("sbuf", [128, 512], "bfloat16"), "grp": ("sbuf", [128, 512], "bfloat16"),
+    "wt": ("sbuf", [128, 2048], "bfloat16"), "w2t": ("sbuf", [128, 2048], "bfloat16"),
+    "xg": ("sbuf", [128, 4 * SL], "bfloat16"), "gt": ("sbuf", [128, 4 * SL], "bfloat16"),
+    "ps": ("psum", [128, 4096], "float32"),
+}
+for _n, _w in (("wq", 512), ("vq", 512), ("xo", CAP), ("go", CAP), ("sx", RM), ("sg", RM), ("lx", RM), ("lg", RM)):
+    SCRATCH[_n + "c"] = ("sbuf", [128, _w], "float8_e4m3fn_x4")
+    SCRATCH[_n + "p"] = ("sbuf", [128, _w], "uint8")
+for _b in range(4):
+    SCRATCH["so%d" % _b] = ("sbuf", [128, SL // 16], "uint16")
+    SCRATCH["z%d" % _b] = ("sbuf", [128, SL], "float32")
+    SCRATCH["zs%d" % _b] = ("sbuf", [128, 256], "float32")
+    SCRATCH["mm%d" % _b] = ("sbuf", [128, 256], "float32")
+    SCRATCH["cw%d" % _b] = ("sbuf", [128, 128], "bfloat16")
+    SCRATCH["ta%d" % _b] = ("sbuf", [128, 256], "bfloat16")
+    SCRATCH["tb%d" % _b] = ("sbuf", [128, 512], "bfloat16")
+    SCRATCH["tg%d" % _b] = ("sbuf", [128, SL], "bfloat16")
+    SCRATCH["u%d" % _b] = ("sbuf", [128, UW], "float32")
+    for _k in range(4):
+        SCRATCH["ac%d%d" % (_b, _k)] = ("sbuf", [128, 256], "float32")
+    SCRATCH["yo%d" % _b] = ("sbuf", [128, 128], "float32")
+
+EVENTS = 146
+SEMAPHORES = ["ax", "ag", "sentx", "sentg"] + ["e%d" % _i for _i in range(EVENTS)]
+
+
+def engine_plan(topo, cores, s):
+    me = cores[s]
+    same = [d for d in range(N) if d != s and topo.die(cores[d]) == topo.die(me)]
+    cross = [d for d in range(N) if d != s and topo.die(cores[d]) != topo.die(me)]
+    es = topo.engines(me, cores[(s + 1) % N])
+    even, odd = es[0::2], es[1::2]
+    plan = {}
+    if len(same) == 1 and len(cross) == 2:
+        h = len(even) // 2
+        plan[same[0]] = (even, odd)
+        plan[cross[0]] = (odd[:h], even[:h])
+        plan[cross[1]] = (odd[h:], even[h:])
+    else:
+        h = len(es) // 4
+        for i, d in enumerate(same + cross):
+            plan[d] = (es[h * i:h * i + h], es[h * i:h * i + h])
+    return plan
+
+
+def rank_program(g, core, T, topo):
+    r = T.rank_of(core)
+    if r is None:
+        return
+    A, Act = AluOpType, ActivationFunctionType
+    cores = list(T.cores)
+    Q = {"g": g, "v": g.vector, "a": g.scalar, "s": g.sync, "t": g.tensor}
+    V, S, Y, TE = g.vector, g.scalar, g.sync, g.tensor
+
+    made, seen = [], set()
+
+    def ev():
+        e = {"k": len(made), "s": T.sem["e%d" % len(made)], "n": 0, "w": False}
+        made.append(e)
+        return e
+
+    def inc(op, e, n=1):
+        op.then_inc(e["s"], n)
+        e["n"] += n
+        return e
+
+    def do(op):
+        return inc(op, ev())
+
+    def need(q, *es):
+        for e in es:
+            if (q, e["k"]) not in seen:
+                seen.add((q, e["k"]))
+                e["w"] = True
+                Q[q].wait_ge(e["s"], e["n"])
+
+    plans = [engine_plan(topo, cores, s) for s in range(N)]
+
+    def bits(es):
+        return sum(1 << e for e in es)
+
+    arrive = sum(len(plans[s][r][0]) + len(plans[s][r][1]) for s in range(N) if s != r)
+    sent = sum(len(a) + len(b) for a, b in plans[r].values())
+
+    def send(src, dst, arrived, left):
+        for part in (0, 1):
+            tr = []
+            for q in (1, 2, 3):
+                d = (r + q) % N
+                rid, pid, _ = topo.addr(cores[d])
+                a, b = CAP * (q - 1), CAP * (3 - q)
+                if part == 0:
+                    f, t = T[src + "c"][:, a:a + CAP].bitcast(dt.uint8), T[dst + "c"][:, b:b + CAP].bitcast(dt.uint8)
+                else:
+                    f, t = T[src + "p"][:, a:a + CAP], T[dst + "p"][:, b:b + CAP]
+                tr.append(RemoteDMATransfer(dst_ids=[DstId(rid=rid, pnc=pid)], dma_engine_mask=bits(plans[r][d][part]),
+                                            remote_sem=arrived, src=f, dst=t))
+            g.remote_dma_fused(tr, local_sem=left)
+
+    e_x, e_sn, e_w, e_dnb, e_nb, e_gr = ev(), ev(), ev(), ev(), ev(), ev()
+    inc(Y.dma_start(T.xt[:, :], T.x[:, :]), e_x, 16)
+    for p in range(4):
+        inc(Y.dma_start(T.snl[16 * p:16 * p + 16, :], T.sn[:, :]), e_sn, 16)
+    for p in range(4, 8):
+        inc(S.dma_start(T.snl[16 * p:16 * p + 16, :], T.sn[:, :]), e_sn, 16)
+    for i, k in enumerate(ORDER):
+        inc(S.dma_start(T.dnb[:, 8 * i:8 * i + 8], T.nb[k:16:4, :]), e_dnb, 16)
+    inc(Y.dma_start(T.wt[:, :], T.w[:, :]), e_w, 16)
+    need("s", e_dnb)
+    for p in range(8):
+        inc(Y.dma_start(T.nbl[16 * p:16 * p + 16, :], T.dnb[:, :]), e_nb, 16)
+    inc(Y.dma_start(T.grt[:, :], T.gr[:, :]), e_gr, 16)
+
+    e_p = do(g.iota(T.pidx[:, 0:1], [[1, 1]], 0, 1))
+    e_tm = do(g.iota(T.tm[:, :], [[0, SL // 16], [1, 16]], 0, 0, allow_small_or_imprecise_dtypes=True))
+    e_gio = do(g.iota(T.gio[:, :], [[1, 4], [16, 8]], 0, 0))
+    e_vals = do(g.iota(T.vals[:, :], [[1, 2], [256, 2], [2, NODES]], 0, 0, allow_small_or_imprecise_dtypes=True))
+    e_inv0 = do(V.memset(T.inv[:, :], 0.0))
+    need("v", e_p)
+    e_p15 = do(V.tensor_scalar(T.p15[:, 0:1], T.pidx[:, 0:1], 15, None, A.bitwise_and))
+    need("v", e_p15)
+    e_p15f = do(V.tensor_copy(T.p15f[:, 0:1], T.p15[:, 0:1]))
+    need("v", e_tm, e_p15f)
+    e_m16 = do(V.tensor_scalar(T.m16[:, :], T.tm[:, :], T.p15f[:, 0:1], None, A.is_equal))
+    e_rr = do(V.tensor_scalar(T.rr[:, :], T.tm[:, :], 1.0, None, A.min))
+
+    need("v", e_sn)
+    e_so = [do(V.tensor_scalar(T["so%d" % t][:, :], T.snl[:, :], 4.0, float(t), A.mult, A.add)) for t in range(4)]
+    runs = [(10 * (r + 1), 40, CAP)] if r < N - 1 else []
+    if r:
+        runs.append((0, 10 * r, CAP * (N - r)))
+
+    def pick(q, t, a, b, pos, e):
+        out = T.xg[:, 4 * pos + t:4 * (pos + 16 * (b - a)):4]
+        win = T.xt[:, 0:512].indirect(T["so%d" % t][:, a:b])
+        inc(S.activation(out, win, Act.Copy) if q == "a" else V.tensor_copy(out, win), e)
+
+    e_xa, e_xv, e_xo = ev(), ev(), ev()
+    need("a", e_x)
+    for t in (0, 1):
+        need("a", e_so[t])
+        for a, b, pos in runs:
+            pick("a", t, a, b, pos, e_xa)
+    need("v", e_x)
+    for t in (2, 3):
+        need("v", e_so[t])
+        for a, b, pos in runs:
+            pick("v", t, a, b, pos, e_xv)
+    need("v", e_xa, e_xv)
+    e_sx = do(V.quantize_mx(T.sxc[:, 0:RM], T.sxp[:, 0:RM], T.xg[:, 4 * CAP:4 * SL]))
+    need("g", e_sx)
+    send("sx", "lx", T.sem.ax, T.sem.sentx)
+
+    for t in range(4):
+        need("a", e_so[t])
+        pick("a", t, 10 * r, 10 * r + 10, 0, e_xo)
+    need("v", e_w)
+    e_wq = do(V.quantize_mx(T.wqc[:, 0:512], T.wqp[:, 0:512], T.wt[:, 0:2048]))
+    need("v", e_nb)
+    if r:
+        e1 = do(V.tensor_scalar(T.nb1[:, :], T.nbl[:, :], float(CAP * r), float(SL), A.is_lt, A.mult))
+    e_p12 = do(V.tensor_scalar(T.p12[:, 0:1], T.pidx[:, 0:1], 12, None, A.bitwise_and))
+    inc(V.tensor_scalar(T.p3[:, 0:1], T.pidx[:, 0:1], 3, None, A.bitwise_and), e_p12)
+    if r:
+        need("v", e1)
+        e2 = do(V.tensor_tensor(T.nb2[:, :], T.nbl[:, :], T.nb1[:, :], A.add))
+    need("v", e_p12)
+    e_p12f = do(V.tensor_copy(T.p12f[:, 0:1], T.p12[:, 0:1]))
+    if r:
+        need("v", e2)
+        e_nbo = do(V.tensor_scalar(T.nbo[:, :], T.nb2[:, :], float(-CAP * r), None, A.add))
+    else:
+        e_nbo = do(V.tensor_copy(T.nbo[:, :], T.nbl[:, :]))
+    need("v", e_p12f)
+    e_ppf = do(V.tensor_scalar(T.ppf[:, 0:1], T.p3[:, 0:1], 128.0, T.p12f[:, 0:1], A.mult, A.add))
+    need("v", e_xo)
+    e_xoq = do(V.quantize_mx(T.xoc[:, 0:CAP], T.xop[:, 0:CAP], T.xg[:, 0:4 * CAP]))
+    need("v", e_gio, e_ppf)
+    e_glo = do(V.tensor_scalar(T.glo[:, :], T.gio[:, :], T.ppf[:, 0:1], None, A.add))
+
+    H = RM // 2
+    BANK = {(0, 0): 0, (0, 1): 1, (1, 0): 2, (2, 0): 3, (3, 0): 4}
+    OWN = (5, 6, 7, 4)
+    last = {}
+
+    def product(bank, st, b, mv, a, w):
+        if bank in last:
+            need("t", last[bank])
+        return do(TE.matmul_mx(T.ps[:, 512 * bank:512 * bank + w], T[st + "c"][:, 128 * b:128 * b + 128], T[st + "p"][:, 128 * b:128 * b + 128],
+                               T[mv + "c"][:, a:a + w], T[mv + "p"][:, a:a + w], True, True))
+
+    def take(q, bank, w, out, e_mm):
+        need(q, e_mm)
+        src = T.ps[:, 512 * bank:512 * bank + w]
+        last[bank] = do(S.activation(out, src, Act.Copy) if q == "a" else V.tensor_copy(out, src))
+        return last[bank]
+
+    need("t", e_wq, e_xoq)
+    e_mo = [product(OWN[b], "wq", b, "xo", 0, CAP) for b in range(4)]
+    e_zo = [take("a", OWN[b], CAP, T["z%d" % b][:, 0:CAP], e_mo[b]) for b in range(4)]
+    need("a", e_gr, e_glo)
+    e_grp = do(S.activation(T.grp[:, :], T.grt[:, 0:512].indirect(T.glo[:, 0:32]), Act.Copy))
+
+    need("v", e_nbo, e_vals, e_inv0)
+    e_sc = do(V.tensor_copy(T.inv[:, 0:SL].indirect(T.nbo[:, 0:32]), T.vals[:, 0:512]))
+    need("v", e_sc, e_m16)
+    e_s1 = do(V.tensor_tensor_scan(T.sc1[:, :], T.inv[:, :], T.m16[:, :], 0.0, A.add, A.mult))
+    need("v", e_s1, e_rr)
+    e_s2 = do(V.tensor_tensor_scan(T.sc2[:, :], T.rr[:, :], T.sc1[:, :], 0.0, A.mult, A.add))
+    need("v", e_s2)
+    e_iv = do(V.tensor_copy(T.iv[:, :], T.sc2[:, 15:SL:16]))
+    e_lt2 = do(V.tensor_copy(T.lt2[:, :], T.sc2[:, 15:SL:16]))
+    need("v", e_iv)
+    e_ivh = do(V.tensor_scalar(T.ivh[:, :], T.iv[:, :], 1, None, A.arith_shift_right))
+    need("v", e_ivh)
+    e_lt1 = do(V.tensor_copy(T.lt1[:, :], T.ivh[:, :]))
+
+    e_dil, e_il, e_w2 = ev(), ev(), ev()
+    g.wait_ge(T.sem.sentx, sent)
+    for q in range(8):
+        inc(g.dma_start(T.dil[2 * q:2 * q + 2, :], T.il[:, q:64:8], allow_slow_non_contiguous=True), e_dil, 16)
+
+    TE.wait_ge(T.sem.ax, arrive)
+    e_mz = {}
+    for (b, h), bank in BANK.items():
+        e_mz[b, h] = product(bank, "wq", b, "lx", H * h, H if b == 0 else RM)
+    need("s", e_mz[0, 0])
+    inc(Y.dma_start(T.w2t[:, :], T.w2[:, :]), e_w2, 16)
+    need("s", e_dil)
+    for p in range(8):
+        inc(Y.dma_start(T.ill[16 * p:16 * p + 16, :], T.dil[:, :]), e_il, 16)
+
+    def rest(q, nm, b, h, e_mm):
+        lo = CAP + H * h
+        return take(q, BANK[b, h], H if b == 0 else RM, T["%s%d" % (nm, b)][:, lo:lo + (H if b == 0 else RM)], e_mm[b, h])
+
+    e_z = {b: [e_zo[b]] for b in range(4)}
+    e_zs, e_cc, e_mm, e_t1, e_t2, e_t2o = {}, {}, {}, {}, {}, {}
+    e_gt, e_go = ev(), ev()
+
+    def odd_gather(b):
+        need("a", e_nbo, *e_z[b])
+        e_zs[b] = do(S.activation(T["zs%d" % b][:, :], T["z%d" % b][:, 0:SL].indirect(T.nbo[:, 16:32]), Act.Copy))
+
+    def compare(b):
+        need("v", e_nbo, e_zs[b], *e_z[b])
+        e_cc[b] = do(V.tensor_tensor(T["tb%d" % b][:, 0:512:2], T["z%d" % b][:, 0:SL].indirect(T.nbo[:, 0:16]), T["zs%d" % b][:, :], A.is_ge))
+        e_mm[b] = do(V.tensor_tensor(T["mm%d" % b][:, :], T["z%d" % b][:, 0:SL].indirect(T.nbo[:, 0:16]), T["zs%d" % b][:, :], A.max))
+
+    def pairs(b):
+        need("v", e_mm[b])
+        m, t = T["mm%d" % b], T["ta%d" % b]
+        e = do(V.tensor_tensor(T["cw%d" % b][:, :], m[:, 0:128], m[:, 128:256], A.is_ge))
+        need("v", e, e_grp)
+        gr = T.grp[:, 128 * b:128 * b + 128]
+        e_a = do(V.tensor_tensor(t[:, 0:128], gr, T["cw%d" % b][:, :], A.mult))
+        need("v", e_a)
+        e_t1[b] = [e_a, do(V.tensor_tensor(t[:, 128:256], gr, t[:, 0:128], A.subtract))]
+
+    def mask(b):
+        need("a", e_cc[b])
+        t = T["tb%d" % b]
+        e = do(S.activation(t[:, 1:512:2], t[:, 0:512:2], Act.Identity, bias=1.0, scale=-1.0))
+        need("a", e, e_lt2)
+        e_t2[b] = do(S.activation(T["tg%d" % b][:, CAP:SL], t[:, 0:512].indirect(T.lt2[:, 10:40]), Act.Copy))
+
+    def grad(b, own):
+        lo, hi = (0, CAP) if own else (CAP, SL)
+        need("v", e_lt1, (e_t2o if own else e_t2)[b], *e_t1[b])
+        inc(V.tensor_tensor(T.gt[:, 4 * lo + b:4 * hi:4], T["ta%d" % b][:, 0:256].indirect(T.lt1[:, lo // 16:hi // 16]),
+                            T["tg%d" % b][:, lo:hi], A.mult), e_go if own else e_gt)
+
+    e_z[0].append(rest("a", "z", 0, 0, e_mz))
+    e_z[0].append(rest("v", "z", 0, 1, e_mz))
+    e_z[1].append(rest("v", "z", 1, 0, e_mz))
+    odd_gather(0)
+    odd_gather(1)
+    compare(0)
+    pairs(0)
+    mask(0)
+    e_z[2].append(rest("a", "z", 2, 0, e_mz))
+    odd_gather(2)
+    compare(1)
+    grad(0, False)
+    pairs(1)
+    mask(1)
+    e_z[3].append(rest("a", "z", 3, 0, e_mz))
+    odd_gather(3)
+    compare(2)
+    grad(1, False)
+    pairs(2)
+    mask(2)
+    compare(3)
+    grad(2, False)
+    pairs(3)
+    mask(3)
+    grad(3, False)
+    need("v", e_gt)
+    e_sg = do(V.quantize_mx(T.sgc[:, 0:RM], T.sgp[:, 0:RM], T.gt[:, 4 * CAP:4 * SL]))
+    need("g", e_sg)
+    send("sg", "lg", T.sem.ag, T.sem.sentg)
+
+    for b in range(4):
+        e_t2o[b] = do(S.activation(T["tg%d" % b][:, 0:CAP], T["tb%d" % b][:, 0:512].indirect(T.lt2[:, 0:10]), Act.Copy))
+    need("v", e_w2)
+    e_vq = do(V.quantize_mx(T.vqc[:, 0:512], T.vqp[:, 0:512], T.w2t[:, 0:2048]))
+    for b in range(4):
+        grad(b, True)
+    need("v", e_go)
+    e_goq = do(V.quantize_mx(T.goc[:, 0:CAP], T.gop[:, 0:CAP], T.gt[:, 0:4 * CAP]))
+    need("v", e_il)
+    e_i1 = do(V.tensor_scalar(T.il1[:, :], T.ill[:, :], float(CAP * r), float(SL), A.is_lt, A.mult))
+    inc(V.tensor_scalar(T.il2[:, :], T.ill[:, :], 0.0, float(CAP * r + 1), A.is_lt, A.mult), e_i1)
+    e_u0 = do(V.memset(T.u0[:, SL:UW], 0.0))
+    need("v", e_i1)
+    e_i3 = do(V.tensor_tensor(T.il3[:, :], T.ill[:, :], T.il1[:, :], A.add))
+    inc(V.memset(T.u1[:, SL:UW], 0.0), e_u0)
+    need("v", e_i3)
+    e_i4 = do(V.tensor_tensor(T.il4[:, :], T.il3[:, :], T.il2[:, :], A.add))
+    inc(V.memset(T.u2[:, SL:UW], 0.0), e_u0)
+    inc(V.memset(T.u3[:, SL:UW], 0.0), e_u0)
+    need("v", e_i4)
+    e_ilo = do(V.tensor_scalar(T.ilo[:, :], T.il4[:, :], float(-CAP * r), None, A.add))
+
+    need("t", e_vq, e_goq)
+    e_mo = [product(OWN[b], "vq", b, "go", 0, CAP) for b in range(4)]
+    e_uo = [take("a", OWN[b], CAP, T["u%d" % b][:, 0:CAP], e_mo[b]) for b in range(4)]
+
+    TE.wait_ge(T.sem.ag, arrive)
+    e_mu = {}
+    for (b, h), bank in BANK.items():
+        e_mu[b, h] = product(bank, "vq", b, "lg", H * h, H if b == 0 else RM)
+    e_u = {b: [e_uo[b], e_u0] for b in range(4)}
+    e_us = {}
+
+    def last_places(b):
+        need("a", e_ilo, *e_u[b])
+        e_us[b] = do(S.activation(T["ac%d0" % b][:, :], T["u%d" % b][:, 0:UW].indirect(T.ilo[:, 48:64]), Act.Copy))
+
+    e_u[0].append(rest("a", "u", 0, 0, e_mu))
+    e_u[0].append(rest("v", "u", 0, 1, e_mu))
+    e_u[1].append(rest("v", "u", 1, 0, e_mu))
+    last_places(0)
+    e_u[2].append(rest("a", "u", 2, 0, e_mu))
+    last_places(1)
+    e_u[3].append(rest("a", "u", 3, 0, e_mu))
+    last_places(2)
+    last_places(3)
+    e_y = ev()
+    for b in range(4):
+        e = e_us[b]
+        need("v", e_ilo, *e_u[b])
+        for i in range(3):
+            need("v", e)
+            e = do(V.tensor_tensor(T["ac%d%d" % (b, i + 1)][:, :], T["u%d" % b][:, 0:UW].indirect(T.ilo[:, 16 * i:16 * i + 16]),
+                                   T["ac%d%d" % (b, i)][:, :], A.add))
+        need("v", e)
+        a = T["ac%d3" % b]
+        e = do(V.tensor_tensor(T["yo%d" % b][:, :], a[:, 0:128], a[:, 128:256], A.add))
+        need("s", e)
+        inc(Y.dma_start(T.y[:, 128 * b:128 * b + 128], T["yo%d" % b][:, :]), e_y, 16)
+    need("s", e_y)
+    g.wait_ge(T.sem.sentg, sent)
+    for e in made:
+        if not e["w"]:
+            need("g", e)

@@ -4,23 +4,19 @@ from concourse.mybir import dt, AluOpType, ActivationFunctionType
 
 N, NODES, CAP, F = 4, 128, 160, 8
 SL = N * CAP
-RM = SL - CAP
+HF = 2 * CAP
 UW = SL + 8
 ORDER = (0, 2, 1, 3)
+STAGES = ((3,), (1, 2))
 
 SCRATCH = {
-    "snl": ("sbuf", [128, SL // 16], "int32"),
-    "nbl": ("sbuf", [128, 32], "int32"), "nb1": ("sbuf", [128, 32], "int32"), "nb2": ("sbuf", [128, 32], "int32"),
-    "nbo": ("sbuf", [128, 32], "uint16"), "dnb": ("dram", [16, 32], "int32"),
-    "ill": ("sbuf", [128, 64], "int32"), "il1": ("sbuf", [128, 64], "int32"), "il2": ("sbuf", [128, 64], "int32"),
-    "il3": ("sbuf", [128, 64], "int32"), "il4": ("sbuf", [128, 64], "int32"),
-    "ilo": ("sbuf", [128, 64], "uint16"), "dil": ("dram", [16, 64], "int32"),
+    "snl": ("sbuf", [128, SL // 16], "int32"), "nbl": ("sbuf", [128, 32], "int32"), "dnb": ("dram", [16, 32], "int32"),
+    "nbo": ("sbuf", [128, 32], "uint16"), "nbi": ("sbuf", [128, 32], "uint16"),
+    "ill": ("sbuf", [128, 64], "int32"), "ilo": ("sbuf", [128, 64], "uint16"), "dil": ("dram", [16, 64], "int32"),
+    "glo": ("sbuf", [128, 32], "uint16"), "gio": ("sbuf", [128, 32], "int32"),
     "pidx": ("sbuf", [128, 1], "int32"), "p12": ("sbuf", [128, 1], "int32"), "p3": ("sbuf", [128, 1], "int32"),
-    "p15": ("sbuf", [128, 1], "int32"), "p12f": ("sbuf", [128, 1], "float32"), "p15f": ("sbuf", [128, 1], "float32"),
-    "ppf": ("sbuf", [128, 1], "float32"), "gio": ("sbuf", [128, 32], "int32"), "glo": ("sbuf", [128, 32], "uint16"),
-    "tm": ("sbuf", [128, SL], "bfloat16"), "m16": ("sbuf", [128, SL], "bfloat16"), "rr": ("sbuf", [128, SL], "bfloat16"),
-    "vals": ("sbuf", [128, 512], "float32"), "inv": ("sbuf", [128, SL], "float32"),
-    "sc1": ("sbuf", [128, SL], "float32"), "sc2": ("sbuf", [128, SL], "float32"),
+    "p12f": ("sbuf", [128, 1], "float32"), "ppf": ("sbuf", [128, 1], "float32"),
+    "vals": ("sbuf", [128, 512], "int32"), "inv": ("sbuf", [128, SL], "int32"),
     "iv": ("sbuf", [128, 40], "int32"), "ivh": ("sbuf", [128, 40], "int32"),
     "lt1": ("sbuf", [128, 40], "uint16"), "lt2": ("sbuf", [128, 40], "uint16"),
     "xt": ("sbuf", [128, 512], "bfloat16"), "grt": ("sbuf", [128, 512], "bfloat16"), "grp": ("sbuf", [128, 512], "bfloat16"),
@@ -28,7 +24,11 @@ SCRATCH = {
     "xg": ("sbuf", [128, 4 * SL], "bfloat16"), "gt": ("sbuf", [128, 4 * SL], "bfloat16"),
     "ps": ("psum", [128, 4096], "float32"),
 }
-for _n, _w in (("wq", 512), ("vq", 512), ("xo", CAP), ("go", CAP), ("sx", RM), ("sg", RM), ("lx", RM), ("lg", RM)):
+for _i in range(1, 8):
+    SCRATCH["nb%d" % _i] = ("sbuf", [128, 32], "int32")
+for _i in range(1, 5):
+    SCRATCH["il%d" % _i] = ("sbuf", [128, 64], "int32")
+for _n, _w in (("wq", 512), ("vq", 512), ("sx", SL), ("sg", SL), ("lx", SL), ("lg", SL)):
     SCRATCH[_n + "c"] = ("sbuf", [128, _w], "float8_e4m3fn_x4")
     SCRATCH[_n + "p"] = ("sbuf", [128, _w], "uint8")
 for _b in range(4):
@@ -45,27 +45,8 @@ for _b in range(4):
         SCRATCH["ac%d%d" % (_b, _k)] = ("sbuf", [128, 256], "float32")
     SCRATCH["yo%d" % _b] = ("sbuf", [128, 128], "float32")
 
-EVENTS = 146
-SEMAPHORES = ["ax", "ag", "sentx", "sentg"] + ["e%d" % _i for _i in range(EVENTS)]
-
-
-def engine_plan(topo, cores, s):
-    me = cores[s]
-    same = [d for d in range(N) if d != s and topo.die(cores[d]) == topo.die(me)]
-    cross = [d for d in range(N) if d != s and topo.die(cores[d]) != topo.die(me)]
-    es = topo.engines(me, cores[(s + 1) % N])
-    even, odd = es[0::2], es[1::2]
-    plan = {}
-    if len(same) == 1 and len(cross) == 2:
-        h = len(even) // 2
-        plan[same[0]] = (even, odd)
-        plan[cross[0]] = (odd[:h], even[:h])
-        plan[cross[1]] = (odd[h:], even[h:])
-    else:
-        h = len(es) // 4
-        for i, d in enumerate(same + cross):
-            plan[d] = (es[h * i:h * i + h], es[h * i:h * i + h])
-    return plan
+EVENTS = 144
+SEMAPHORES = ["ax0", "ax1", "ag0", "ag1", "sentx", "sentg"] + ["e%d" % _i for _i in range(EVENTS)]
 
 
 def rank_program(g, core, T, topo):
@@ -99,28 +80,30 @@ def rank_program(g, core, T, topo):
                 e["w"] = True
                 Q[q].wait_ge(e["s"], e["n"])
 
-    plans = [engine_plan(topo, cores, s) for s in range(N)]
+    def share(s, q):
+        es = topo.engines(cores[s], cores[(s + q) % N])
+        return (es[1::2], es[0::2]) if q == 1 else (es[0::2], es[1::2])
 
-    def bits(es):
-        return sum(1 << e for e in es)
+    def count(s, q):
+        return sum(len(es) for es in share(s, q))
 
-    arrive = sum(len(plans[s][r][0]) + len(plans[s][r][1]) for s in range(N) if s != r)
-    sent = sum(len(a) + len(b) for a, b in plans[r].values())
-
-    def send(src, dst, arrived, left):
+    def send(src, dst, stage, arrived, left):
         for part in (0, 1):
             tr = []
-            for q in (1, 2, 3):
+            for q in STAGES[stage]:
                 d = (r + q) % N
                 rid, pid, _ = topo.addr(cores[d])
-                a, b = CAP * (q - 1), CAP * (3 - q)
+                a, b = CAP * q, CAP * (N - q)
                 if part == 0:
                     f, t = T[src + "c"][:, a:a + CAP].bitcast(dt.uint8), T[dst + "c"][:, b:b + CAP].bitcast(dt.uint8)
                 else:
                     f, t = T[src + "p"][:, a:a + CAP], T[dst + "p"][:, b:b + CAP]
-                tr.append(RemoteDMATransfer(dst_ids=[DstId(rid=rid, pnc=pid)], dma_engine_mask=bits(plans[r][d][part]),
+                tr.append(RemoteDMATransfer(dst_ids=[DstId(rid=rid, pnc=pid)], dma_engine_mask=sum(1 << e for e in share(r, q)[part]),
                                             remote_sem=arrived, src=f, dst=t))
             g.remote_dma_fused(tr, local_sem=left)
+
+    arrive = [sum(count((r - q) % N, q) for q in st) for st in STAGES]
+    sent = sum(count(r, q) for st in STAGES for q in st)
 
     e_x, e_sn, e_w, e_dnb, e_nb, e_gr = ev(), ev(), ev(), ev(), ev(), ev()
     inc(Y.dma_start(T.xt[:, :], T.x[:, :]), e_x, 16)
@@ -130,82 +113,108 @@ def rank_program(g, core, T, topo):
         inc(S.dma_start(T.snl[16 * p:16 * p + 16, :], T.sn[:, :]), e_sn, 16)
     for i, k in enumerate(ORDER):
         inc(S.dma_start(T.dnb[:, 8 * i:8 * i + 8], T.nb[k:16:4, :]), e_dnb, 16)
-    inc(Y.dma_start(T.wt[:, :], T.w[:, :]), e_w, 16)
+    inc(S.dma_start(T.wt[:, :], T.w[:, :]), e_w, 16)
     need("s", e_dnb)
     for p in range(8):
         inc(Y.dma_start(T.nbl[16 * p:16 * p + 16, :], T.dnb[:, :]), e_nb, 16)
     inc(Y.dma_start(T.grt[:, :], T.gr[:, :]), e_gr, 16)
 
-    e_p = do(g.iota(T.pidx[:, 0:1], [[1, 1]], 0, 1))
-    e_tm = do(g.iota(T.tm[:, :], [[0, SL // 16], [1, 16]], 0, 0, allow_small_or_imprecise_dtypes=True))
-    e_gio = do(g.iota(T.gio[:, :], [[1, 4], [16, 8]], 0, 0))
-    e_vals = do(g.iota(T.vals[:, :], [[1, 2], [256, 2], [2, NODES]], 0, 0, allow_small_or_imprecise_dtypes=True))
-    e_inv0 = do(V.memset(T.inv[:, :], 0.0))
+    e_p, e_zero, e_p12 = ev(), ev(), ev()
+    inc(g.iota(T.pidx[:, 0:1], [[1, 1]], 0, 1), e_p)
+    inc(g.iota(T.gio[:, :], [[1, 4], [16, 8]], 0, 0), e_p)
+    e_vals = do(g.iota(T.vals[:, :], [[1, 2], [256, 2], [2, NODES]], 0, 0))
+    inc(V.memset(T.inv[:, :], 0), e_zero)
     need("v", e_p)
-    e_p15 = do(V.tensor_scalar(T.p15[:, 0:1], T.pidx[:, 0:1], 15, None, A.bitwise_and))
-    need("v", e_p15)
-    e_p15f = do(V.tensor_copy(T.p15f[:, 0:1], T.p15[:, 0:1]))
-    need("v", e_tm, e_p15f)
-    e_m16 = do(V.tensor_scalar(T.m16[:, :], T.tm[:, :], T.p15f[:, 0:1], None, A.is_equal))
-    e_rr = do(V.tensor_scalar(T.rr[:, :], T.tm[:, :], 1.0, None, A.min))
+    inc(V.tensor_scalar(T.p12[:, 0:1], T.pidx[:, 0:1], 12, None, A.bitwise_and), e_p12)
+    inc(V.tensor_scalar(T.p3[:, 0:1], T.pidx[:, 0:1], 3, None, A.bitwise_and), e_p12)
+    inc(V.memset(T.u0[:, SL:UW], 0.0), e_zero)
+    need("v", e_p12)
+    e_p12f = do(V.tensor_copy(T.p12f[:, 0:1], T.p12[:, 0:1]))
+    inc(V.memset(T.u1[:, SL:UW], 0.0), e_zero)
+    need("v", e_p12f)
+    e_ppf = do(V.tensor_scalar(T.ppf[:, 0:1], T.p3[:, 0:1], 128.0, T.p12f[:, 0:1], A.mult, A.add))
+    inc(V.memset(T.u2[:, SL:UW], 0.0), e_zero)
+    need("v", e_ppf)
+    e_glo = do(V.tensor_scalar(T.glo[:, :], T.gio[:, :], T.ppf[:, 0:1], None, A.add))
+    inc(V.memset(T.u3[:, SL:UW], 0.0), e_zero)
 
     need("v", e_sn)
-    e_so = [do(V.tensor_scalar(T["so%d" % t][:, :], T.snl[:, :], 4.0, float(t), A.mult, A.add)) for t in range(4)]
-    runs = [(10 * (r + 1), 40, CAP)] if r < N - 1 else []
-    if r:
-        runs.append((0, 10 * r, CAP * (N - r)))
+    e_so = [ev(), ev(), ev()]
+    e_so.append(e_so[2])
+    for t in range(4):
+        inc(V.tensor_scalar(T["so%d" % t][:, :], T.snl[:, :], 4.0, float(t), A.mult, A.add), e_so[t])
 
-    def pick(q, t, a, b, pos, e):
-        out = T.xg[:, 4 * pos + t:4 * (pos + 16 * (b - a)):4]
-        win = T.xt[:, 0:512].indirect(T["so%d" % t][:, a:b])
-        inc(S.activation(out, win, Act.Copy) if q == "a" else V.tensor_copy(out, win), e)
+    def pick(q, t, runs, e):
+        pos, at = CAP * runs[0], [(r + i) % N for i in runs]
+        parts = [(at[0], len(at))] if at[-1] - at[0] == len(at) - 1 else [(d, 1) for d in at]
+        for d, n in parts:
+            out = T.xg[:, 4 * pos + t:4 * (pos + n * CAP):4]
+            win = T.xt[:, 0:512].indirect(T["so%d" % t][:, 10 * d:10 * (d + n)])
+            inc(S.activation(out, win, Act.Copy) if q == "a" else V.tensor_copy(out, win), e)
+            pos += n * CAP
 
-    e_xa, e_xv, e_xo = ev(), ev(), ev()
+    def pack(dst, src, runs):
+        a, b = CAP * runs[0], CAP * (runs[-1] + 1)
+        return do(V.quantize_mx(T[dst + "c"][:, a:b], T[dst + "p"][:, a:b], T[src][:, 4 * a:4 * b]))
+
     need("a", e_x)
-    for t in (0, 1):
-        need("a", e_so[t])
-        for a, b, pos in runs:
-            pick("a", t, a, b, pos, e_xa)
     need("v", e_x)
-    for t in (2, 3):
-        need("v", e_so[t])
-        for a, b, pos in runs:
-            pick("v", t, a, b, pos, e_xv)
-    need("v", e_xa, e_xv)
-    e_sx = do(V.quantize_mx(T.sxc[:, 0:RM], T.sxp[:, 0:RM], T.xg[:, 4 * CAP:4 * SL]))
-    need("g", e_sx)
-    send("sx", "lx", T.sem.ax, T.sem.sentx)
+    for stage, runs in enumerate(STAGES):
+        e_g = ev()
+        for t in (0, 1):
+            need("a", e_so[t])
+            pick("a", t, runs, e_g)
+        for t in (2, 3):
+            need("v", e_so[t])
+            pick("v", t, runs, e_g)
+        need("v", e_g)
+        need("g", pack("sx", "xg", runs))
+        send("sx", "lx", stage, T.sem["ax%d" % stage], T.sem.sentx)
 
+    e_xo = ev()
     for t in range(4):
         need("a", e_so[t])
-        pick("a", t, 10 * r, 10 * r + 10, 0, e_xo)
+        pick("a", t, (0,), e_xo)
+    need("a", e_gr, e_glo)
+    e_grp = do(S.activation(T.grp[:, :], T.grt[:, 0:512].indirect(T.glo[:, 0:32]), Act.Copy))
     need("v", e_w)
     e_wq = do(V.quantize_mx(T.wqc[:, 0:512], T.wqp[:, 0:512], T.wt[:, 0:2048]))
     need("v", e_nb)
+    rel = T.nbl
     if r:
-        e1 = do(V.tensor_scalar(T.nb1[:, :], T.nbl[:, :], float(CAP * r), float(SL), A.is_lt, A.mult))
-    e_p12 = do(V.tensor_scalar(T.p12[:, 0:1], T.pidx[:, 0:1], 12, None, A.bitwise_and))
-    inc(V.tensor_scalar(T.p3[:, 0:1], T.pidx[:, 0:1], 3, None, A.bitwise_and), e_p12)
-    if r:
-        need("v", e1)
-        e2 = do(V.tensor_tensor(T.nb2[:, :], T.nbl[:, :], T.nb1[:, :], A.add))
-    need("v", e_p12)
-    e_p12f = do(V.tensor_copy(T.p12f[:, 0:1], T.p12[:, 0:1]))
-    if r:
-        need("v", e2)
-        e_nbo = do(V.tensor_scalar(T.nbo[:, :], T.nb2[:, :], float(-CAP * r), None, A.add))
-    else:
-        e_nbo = do(V.tensor_copy(T.nbo[:, :], T.nbl[:, :]))
-    need("v", e_p12f)
-    e_ppf = do(V.tensor_scalar(T.ppf[:, 0:1], T.p3[:, 0:1], 128.0, T.p12f[:, 0:1], A.mult, A.add))
+        e = do(V.tensor_scalar(T.nb1[:, :], T.nbl[:, :], float(CAP * r), float(SL), A.is_lt, A.mult))
+        need("v", e)
+        e = do(V.tensor_tensor(T.nb2[:, :], T.nbl[:, :], T.nb1[:, :], A.add))
+        need("v", e)
+        e = do(V.tensor_scalar(T.nb3[:, :], T.nb2[:, :], float(-CAP * r), None, A.add))
+        need("v", e)
+        rel = T.nb3
+    e_4 = do(V.tensor_scalar(T.nb4[:, :], rel[:, :], 4, None, A.arith_shift_right))
+    e_nbo = do(V.tensor_copy(T.nbo[:, :], rel[:, :]))
+    e_56 = do(V.tensor_scalar(T.nb5[:, :], rel[:, :], 40.0, None, A.mult))
+    need("v", e_4)
+    inc(V.tensor_scalar(T.nb6[:, :], T.nb4[:, :], -639.0, None, A.mult), e_56)
     need("v", e_xo)
-    e_xoq = do(V.quantize_mx(T.xoc[:, 0:CAP], T.xop[:, 0:CAP], T.xg[:, 0:4 * CAP]))
-    need("v", e_gio, e_ppf)
-    e_glo = do(V.tensor_scalar(T.glo[:, :], T.gio[:, :], T.ppf[:, 0:1], None, A.add))
+    e_xoq = pack("lx", "xg", (0,))
+    need("v", e_56)
+    e = do(V.tensor_tensor(T.nb7[:, :], T.nb5[:, :], T.nb6[:, :], A.add))
+    need("v", e)
+    e = do(V.tensor_copy(T.nbi[:, :], T.nb7[:, :]))
+    need("v", e, e_vals, e_zero)
+    e_sc = do(V.tensor_copy(T.inv[:, 0:SL].indirect(T.nbi[:, 0:32]), T.vals[:, 0:512]))
+    e_iv = ev()
+    need("s", e_sc)
+    for p in range(8):
+        inc(Y.dma_start(T.iv[16 * p:16 * p + 16, :], T.inv[16 * p:16 * p + 1, :]), e_iv, 16)
 
-    H = RM // 2
+    e_dil, e_il, e_w2 = ev(), ev(), ev()
+    g.wait_ge(T.sem.sentx, sent)
+    need("g", e_iv)
+    for q in range(8):
+        inc(g.dma_start(T.dil[2 * q:2 * q + 2, :], T.il[:, q:64:8], allow_slow_non_contiguous=True), e_dil, 16)
+
     BANK = {(0, 0): 0, (0, 1): 1, (1, 0): 2, (2, 0): 3, (3, 0): 4}
-    OWN = (5, 6, 7, 4)
+    FIRST = (5, 6, 7, 4)
     last = {}
 
     def product(bank, st, b, mv, a, w):
@@ -220,170 +229,171 @@ def rank_program(g, core, T, topo):
         last[bank] = do(S.activation(out, src, Act.Copy) if q == "a" else V.tensor_copy(out, src))
         return last[bank]
 
+    def first(st, mv, to):
+        e = [product(FIRST[b], st, b, mv, 0, HF) for b in range(4)]
+        return {b: [take("a", FIRST[b], HF, T["%s%d" % (to, b)][:, 0:HF], e[b])] for b in range(4)}
+
+    def second(st, mv):
+        return {bh: product(bank, st, bh[0], mv, HF + CAP * bh[1], CAP if bh[0] == 0 else HF) for bh, bank in BANK.items()}
+
+    def rest(q, to, b, h, e_mm):
+        lo, w = HF + CAP * h, CAP if b == 0 else HF
+        return take(q, BANK[b, h], w, T["%s%d" % (to, b)][:, lo:lo + w], e_mm[b, h])
+
     need("t", e_wq, e_xoq)
-    e_mo = [product(OWN[b], "wq", b, "xo", 0, CAP) for b in range(4)]
-    e_zo = [take("a", OWN[b], CAP, T["z%d" % b][:, 0:CAP], e_mo[b]) for b in range(4)]
-    need("a", e_gr, e_glo)
-    e_grp = do(S.activation(T.grp[:, :], T.grt[:, 0:512].indirect(T.glo[:, 0:32]), Act.Copy))
-
-    need("v", e_nbo, e_vals, e_inv0)
-    e_sc = do(V.tensor_copy(T.inv[:, 0:SL].indirect(T.nbo[:, 0:32]), T.vals[:, 0:512]))
-    need("v", e_sc, e_m16)
-    e_s1 = do(V.tensor_tensor_scan(T.sc1[:, :], T.inv[:, :], T.m16[:, :], 0.0, A.add, A.mult))
-    need("v", e_s1, e_rr)
-    e_s2 = do(V.tensor_tensor_scan(T.sc2[:, :], T.rr[:, :], T.sc1[:, :], 0.0, A.mult, A.add))
-    need("v", e_s2)
-    e_iv = do(V.tensor_copy(T.iv[:, :], T.sc2[:, 15:SL:16]))
-    e_lt2 = do(V.tensor_copy(T.lt2[:, :], T.sc2[:, 15:SL:16]))
-    need("v", e_iv)
-    e_ivh = do(V.tensor_scalar(T.ivh[:, :], T.iv[:, :], 1, None, A.arith_shift_right))
-    need("v", e_ivh)
-    e_lt1 = do(V.tensor_copy(T.lt1[:, :], T.ivh[:, :]))
-
-    e_dil, e_il, e_w2 = ev(), ev(), ev()
-    g.wait_ge(T.sem.sentx, sent)
-    for q in range(8):
-        inc(g.dma_start(T.dil[2 * q:2 * q + 2, :], T.il[:, q:64:8], allow_slow_non_contiguous=True), e_dil, 16)
-
-    TE.wait_ge(T.sem.ax, arrive)
-    e_mz = {}
-    for (b, h), bank in BANK.items():
-        e_mz[b, h] = product(bank, "wq", b, "lx", H * h, H if b == 0 else RM)
+    TE.wait_ge(T.sem.ax0, arrive[0])
+    e_z = first("wq", "lx", "z")
+    TE.wait_ge(T.sem.ax1, arrive[1])
+    e_mz = second("wq", "lx")
     need("s", e_mz[0, 0])
     inc(Y.dma_start(T.w2t[:, :], T.w2[:, :]), e_w2, 16)
     need("s", e_dil)
     for p in range(8):
         inc(Y.dma_start(T.ill[16 * p:16 * p + 16, :], T.dil[:, :]), e_il, 16)
 
-    def rest(q, nm, b, h, e_mm):
-        lo = CAP + H * h
-        return take(q, BANK[b, h], H if b == 0 else RM, T["%s%d" % (nm, b)][:, lo:lo + (H if b == 0 else RM)], e_mm[b, h])
+    e_zs, e_cc, e_mm, e_c, e_a, e_b, e_cm, e_t2, e_t2o = {}, {}, {}, {}, {}, {}, {}, {}, {}
 
-    e_z = {b: [e_zo[b]] for b in range(4)}
-    e_zs, e_cc, e_mm, e_t1, e_t2, e_t2o = {}, {}, {}, {}, {}, {}
-    e_gt, e_go = ev(), ev()
-
-    def odd_gather(b):
+    def zs(b):
         need("a", e_nbo, *e_z[b])
         e_zs[b] = do(S.activation(T["zs%d" % b][:, :], T["z%d" % b][:, 0:SL].indirect(T.nbo[:, 16:32]), Act.Copy))
 
-    def compare(b):
+    def cc(b):
         need("v", e_nbo, e_zs[b], *e_z[b])
         e_cc[b] = do(V.tensor_tensor(T["tb%d" % b][:, 0:512:2], T["z%d" % b][:, 0:SL].indirect(T.nbo[:, 0:16]), T["zs%d" % b][:, :], A.is_ge))
+
+    def mm(b):
         e_mm[b] = do(V.tensor_tensor(T["mm%d" % b][:, :], T["z%d" % b][:, 0:SL].indirect(T.nbo[:, 0:16]), T["zs%d" % b][:, :], A.max))
 
-    def pairs(b):
+    def c(b):
         need("v", e_mm[b])
-        m, t = T["mm%d" % b], T["ta%d" % b]
-        e = do(V.tensor_tensor(T["cw%d" % b][:, :], m[:, 0:128], m[:, 128:256], A.is_ge))
-        need("v", e, e_grp)
-        gr = T.grp[:, 128 * b:128 * b + 128]
-        e_a = do(V.tensor_tensor(t[:, 0:128], gr, T["cw%d" % b][:, :], A.mult))
-        need("v", e_a)
-        e_t1[b] = [e_a, do(V.tensor_tensor(t[:, 128:256], gr, t[:, 0:128], A.subtract))]
+        e_c[b] = do(V.tensor_tensor(T["cw%d" % b][:, :], T["mm%d" % b][:, 0:128], T["mm%d" % b][:, 128:256], A.is_ge))
 
-    def mask(b):
+    def ta(b):
+        need("v", e_c[b], e_grp)
+        e_a[b] = do(V.tensor_tensor(T["ta%d" % b][:, 0:128], T.grp[:, 128 * b:128 * b + 128], T["cw%d" % b][:, :], A.mult))
+
+    def tb(b):
+        need("v", e_a[b])
+        e_b[b] = do(V.tensor_tensor(T["ta%d" % b][:, 128:256], T.grp[:, 128 * b:128 * b + 128], T["ta%d" % b][:, 0:128], A.subtract))
+
+    def lists():
+        need("v", e_iv)
+        e_l = do(V.tensor_scalar(T.ivh[:, :], T.iv[:, :], 1, None, A.arith_shift_right))
+        e = do(V.tensor_copy(T.lt2[:, :], T.iv[:, :]))
+        need("v", e_l)
+        return inc(V.tensor_copy(T.lt1[:, :], T.ivh[:, :]), e)
+
+    def other(b):
         need("a", e_cc[b])
-        t = T["tb%d" % b]
-        e = do(S.activation(t[:, 1:512:2], t[:, 0:512:2], Act.Identity, bias=1.0, scale=-1.0))
-        need("a", e, e_lt2)
-        e_t2[b] = do(S.activation(T["tg%d" % b][:, CAP:SL], t[:, 0:512].indirect(T.lt2[:, 10:40]), Act.Copy))
+        e_cm[b] = do(S.activation(T["tb%d" % b][:, 1:512:2], T["tb%d" % b][:, 0:512:2], Act.Identity, bias=1.0, scale=-1.0))
 
-    def grad(b, own):
-        lo, hi = (0, CAP) if own else (CAP, SL)
-        need("v", e_lt1, (e_t2o if own else e_t2)[b], *e_t1[b])
+    def t2(b, lo, hi, to):
+        need("a", e_cm[b], e_lt)
+        to[b] = do(S.activation(T["tg%d" % b][:, lo:hi], T["tb%d" % b][:, 0:512].indirect(T.lt2[:, lo // 16:hi // 16]), Act.Copy))
+
+    def grad(b, lo, hi, e):
+        need("v", e_lt, (e_t2 if lo else e_t2o)[b], e_a[b], e_b[b])
         inc(V.tensor_tensor(T.gt[:, 4 * lo + b:4 * hi:4], T["ta%d" % b][:, 0:256].indirect(T.lt1[:, lo // 16:hi // 16]),
-                            T["tg%d" % b][:, lo:hi], A.mult), e_go if own else e_gt)
+                            T["tg%d" % b][:, lo:hi], A.mult), e)
 
     e_z[0].append(rest("a", "z", 0, 0, e_mz))
     e_z[0].append(rest("v", "z", 0, 1, e_mz))
-    e_z[1].append(rest("v", "z", 1, 0, e_mz))
-    odd_gather(0)
-    odd_gather(1)
-    compare(0)
-    pairs(0)
-    mask(0)
-    e_z[2].append(rest("a", "z", 2, 0, e_mz))
-    odd_gather(2)
-    compare(1)
-    grad(0, False)
-    pairs(1)
-    mask(1)
-    e_z[3].append(rest("a", "z", 3, 0, e_mz))
-    odd_gather(3)
-    compare(2)
-    grad(1, False)
-    pairs(2)
-    mask(2)
-    compare(3)
-    grad(2, False)
-    pairs(3)
-    mask(3)
-    grad(3, False)
-    need("v", e_gt)
-    e_sg = do(V.quantize_mx(T.sgc[:, 0:RM], T.sgp[:, 0:RM], T.gt[:, 4 * CAP:4 * SL]))
-    need("g", e_sg)
-    send("sg", "lg", T.sem.ag, T.sem.sentg)
+    zs(0)
+    for b in (1, 2, 3):
+        e_z[b].append(rest("a", "z", b, 0, e_mz))
+        zs(b)
+    cc(0)
+    mm(0)
+    cc(1)
+    c(0)
+    mm(1)
+    ta(0)
+    c(1)
+    tb(0)
+    cc(2)
+    ta(1)
+    e_lt = lists()
+    mm(2)
+    tb(1)
+    c(2)
+    cc(3)
+    ta(2)
+    mm(3)
+    tb(2)
+    c(3)
+    for b in range(4):
+        other(b)
+        t2(b, CAP, SL, e_t2)
+    B3 = 3 * CAP
+    e_g3, e_g12, e_g0 = ev(), ev(), ev()
+    grad(0, CAP, SL, e_g3)
+    ta(3)
+    grad(1, CAP, SL, e_g3)
+    tb(3)
+    grad(2, CAP, SL, e_g3)
+    grad(3, B3, SL, e_g3)
+    need("v", e_g3)
+    need("g", pack("sg", "gt", STAGES[0]))
+    send("sg", "lg", 0, T.sem.ag0, T.sem.sentg)
+    grad(3, CAP, B3, e_g12)
+    need("v", e_g12)
+    need("g", pack("sg", "gt", STAGES[1]))
+    send("sg", "lg", 1, T.sem.ag1, T.sem.sentg)
 
     for b in range(4):
-        e_t2o[b] = do(S.activation(T["tg%d" % b][:, 0:CAP], T["tb%d" % b][:, 0:512].indirect(T.lt2[:, 0:10]), Act.Copy))
+        t2(b, 0, CAP, e_t2o)
+    for b in range(4):
+        grad(b, 0, CAP, e_g0)
     need("v", e_w2)
     e_vq = do(V.quantize_mx(T.vqc[:, 0:512], T.vqp[:, 0:512], T.w2t[:, 0:2048]))
-    for b in range(4):
-        grad(b, True)
-    need("v", e_go)
-    e_goq = do(V.quantize_mx(T.goc[:, 0:CAP], T.gop[:, 0:CAP], T.gt[:, 0:4 * CAP]))
+    need("v", e_g0)
+    e_goq = pack("lg", "gt", (0,))
     need("v", e_il)
     e_i1 = do(V.tensor_scalar(T.il1[:, :], T.ill[:, :], float(CAP * r), float(SL), A.is_lt, A.mult))
-    inc(V.tensor_scalar(T.il2[:, :], T.ill[:, :], 0.0, float(CAP * r + 1), A.is_lt, A.mult), e_i1)
-    e_u0 = do(V.memset(T.u0[:, SL:UW], 0.0))
+    e_i2 = do(V.tensor_scalar(T.il2[:, :], T.ill[:, :], 0.0, float(CAP * r + 1), A.is_lt, A.mult))
     need("v", e_i1)
-    e_i3 = do(V.tensor_tensor(T.il3[:, :], T.ill[:, :], T.il1[:, :], A.add))
-    inc(V.memset(T.u1[:, SL:UW], 0.0), e_u0)
-    need("v", e_i3)
-    e_i4 = do(V.tensor_tensor(T.il4[:, :], T.il3[:, :], T.il2[:, :], A.add))
-    inc(V.memset(T.u2[:, SL:UW], 0.0), e_u0)
-    inc(V.memset(T.u3[:, SL:UW], 0.0), e_u0)
-    need("v", e_i4)
+    inc(V.tensor_tensor(T.il3[:, :], T.ill[:, :], T.il1[:, :], A.add), e_i2)
+    need("v", e_i2)
+    e = do(V.tensor_tensor(T.il4[:, :], T.il3[:, :], T.il2[:, :], A.add))
+    need("v", e)
     e_ilo = do(V.tensor_scalar(T.ilo[:, :], T.il4[:, :], float(-CAP * r), None, A.add))
 
     need("t", e_vq, e_goq)
-    e_mo = [product(OWN[b], "vq", b, "go", 0, CAP) for b in range(4)]
-    e_uo = [take("a", OWN[b], CAP, T["u%d" % b][:, 0:CAP], e_mo[b]) for b in range(4)]
+    TE.wait_ge(T.sem.ag0, arrive[0])
+    e_u = first("vq", "lg", "u")
+    TE.wait_ge(T.sem.ag1, arrive[1])
+    e_mu = second("vq", "lg")
 
-    TE.wait_ge(T.sem.ag, arrive)
-    e_mu = {}
-    for (b, h), bank in BANK.items():
-        e_mu[b, h] = product(bank, "vq", b, "lg", H * h, H if b == 0 else RM)
-    e_u = {b: [e_uo[b], e_u0] for b in range(4)}
-    e_us = {}
+    e_ac = {}
 
-    def last_places(b):
-        need("a", e_ilo, *e_u[b])
-        e_us[b] = do(S.activation(T["ac%d0" % b][:, :], T["u%d" % b][:, 0:UW].indirect(T.ilo[:, 48:64]), Act.Copy))
+    def us(b):
+        need("a", e_ilo, e_zero, *e_u[b])
+        e_ac[b] = do(S.activation(T["ac%d0" % b][:, :], T["u%d" % b][:, 0:UW].indirect(T.ilo[:, 48:64]), Act.Copy))
+
+    def add(b, i):
+        need("v", e_ilo, e_ac[b], *e_u[b])
+        e_ac[b] = do(V.tensor_tensor(T["ac%d%d" % (b, i + 1)][:, :], T["u%d" % b][:, 0:UW].indirect(T.ilo[:, 16 * i:16 * i + 16]),
+                                     T["ac%d%d" % (b, i)][:, :], A.add))
+
+    e_y = ev()
+
+    def out(b):
+        need("v", e_ac[b])
+        e = do(V.tensor_tensor(T["yo%d" % b][:, :], T["ac%d3" % b][:, 0:128], T["ac%d3" % b][:, 128:256], A.add))
+        need("s", e)
+        inc(Y.dma_start(T.y[:, 128 * b:128 * b + 128], T["yo%d" % b][:, :]), e_y, 16)
 
     e_u[0].append(rest("a", "u", 0, 0, e_mu))
     e_u[0].append(rest("v", "u", 0, 1, e_mu))
-    e_u[1].append(rest("v", "u", 1, 0, e_mu))
-    last_places(0)
-    e_u[2].append(rest("a", "u", 2, 0, e_mu))
-    last_places(1)
-    e_u[3].append(rest("a", "u", 3, 0, e_mu))
-    last_places(2)
-    last_places(3)
-    e_y = ev()
-    for b in range(4):
-        e = e_us[b]
-        need("v", e_ilo, *e_u[b])
-        for i in range(3):
-            need("v", e)
-            e = do(V.tensor_tensor(T["ac%d%d" % (b, i + 1)][:, :], T["u%d" % b][:, 0:UW].indirect(T.ilo[:, 16 * i:16 * i + 16]),
-                                   T["ac%d%d" % (b, i)][:, :], A.add))
-        need("v", e)
-        a = T["ac%d3" % b]
-        e = do(V.tensor_tensor(T["yo%d" % b][:, :], a[:, 0:128], a[:, 128:256], A.add))
-        need("s", e)
-        inc(Y.dma_start(T.y[:, 128 * b:128 * b + 128], T["yo%d" % b][:, :]), e_y, 16)
+    us(0)
+    for b in (1, 2, 3):
+        e_u[b].append(rest("a", "u", b, 0, e_mu))
+        us(b)
+    for b, i in ((0, 0), (0, 1), (1, 0), (0, 2), (1, 1), (0, 3), (1, 2), (2, 0), (1, 3), (2, 1), (3, 0), (2, 2), (3, 1), (2, 3), (3, 2), (3, 3)):
+        if i < 3:
+            add(b, i)
+        else:
+            out(b)
     need("s", e_y)
     g.wait_ge(T.sem.sentg, sent)
     for e in made:

@@ -6,28 +6,30 @@ N, NODES, CAP, F = 4, 128, 160, 8
 SL = N * CAP
 HF = 2 * CAP
 UW = SL + 8
+TR = 3 * 2 * NODES
 ORDER = (0, 2, 1, 3)
-STAGES = ((3,), (1, 2))
 
 SCRATCH = {
     "snl": ("sbuf", [128, SL // 16], "int32"), "nbl": ("sbuf", [128, 32], "int32"), "dnb": ("dram", [16, 32], "int32"),
     "nbo": ("sbuf", [128, 32], "uint16"), "nbi": ("sbuf", [128, 32], "uint16"),
     "ill": ("sbuf", [128, 64], "int32"), "ilo": ("sbuf", [128, 64], "uint16"), "dil": ("dram", [16, 64], "int32"),
+    "iln": ("sbuf", [128, 64], "int32"), "ilp": ("sbuf", [128, 64], "uint16"),
     "glo": ("sbuf", [128, 32], "uint16"), "gio": ("sbuf", [128, 32], "int32"),
     "pidx": ("sbuf", [128, 1], "int32"), "p12": ("sbuf", [128, 1], "int32"), "p3": ("sbuf", [128, 1], "int32"),
     "p12f": ("sbuf", [128, 1], "float32"), "ppf": ("sbuf", [128, 1], "float32"),
     "vals": ("sbuf", [128, 512], "int32"), "inv": ("sbuf", [128, SL], "int32"),
-    "iv": ("sbuf", [128, 40], "int32"), "ivh": ("sbuf", [128, 40], "int32"),
-    "lt1": ("sbuf", [128, 40], "uint16"), "lt2": ("sbuf", [128, 40], "uint16"),
-    "xt": ("sbuf", [128, 512], "bfloat16"), "grt": ("sbuf", [128, 512], "bfloat16"), "grp": ("sbuf", [128, 512], "bfloat16"),
+    "iv": ("sbuf", [128, 40], "int32"), "lt": ("sbuf", [128, 40], "uint16"),
+    "xt": ("sbuf", [128, 512], "bfloat16"), "grt": ("sbuf", [128, 512], "bfloat16"),
     "wt": ("sbuf", [128, 2048], "bfloat16"), "w2t": ("sbuf", [128, 2048], "bfloat16"),
     "xg": ("sbuf", [128, 4 * SL], "bfloat16"), "gt": ("sbuf", [128, 4 * SL], "bfloat16"),
+    "d0": ("sbuf", [128, 4 * TR], "bfloat16"), "d1": ("sbuf", [128, 4 * TR], "bfloat16"),
+    "mk": ("sbuf", [128, TR], "bfloat16"), "gb": ("sbuf", [128, 8 * TR], "bfloat16"),
+    "rs": ("sbuf", [128, F * NODES], "float32"),
+    "uu": ("sbuf", [128, 4 * UW], "float32"),
     "ps": ("psum", [128, 4096], "float32"),
 }
-for _i in range(1, 8):
+for _i in range(4, 8):
     SCRATCH["nb%d" % _i] = ("sbuf", [128, 32], "int32")
-for _i in range(1, 5):
-    SCRATCH["il%d" % _i] = ("sbuf", [128, 64], "int32")
 for _n, _w in (("wq", 512), ("vq", 512), ("sx", SL), ("sg", SL), ("lx", SL), ("lg", SL)):
     SCRATCH[_n + "c"] = ("sbuf", [128, _w], "float8_e4m3fn_x4")
     SCRATCH[_n + "p"] = ("sbuf", [128, _w], "uint8")
@@ -36,13 +38,12 @@ for _b in range(4):
     SCRATCH["z%d" % _b] = ("sbuf", [128, SL], "float32")
     SCRATCH["zs%d" % _b] = ("sbuf", [128, 256], "float32")
     SCRATCH["mm%d" % _b] = ("sbuf", [128, 256], "float32")
-    SCRATCH["cw%d" % _b] = ("sbuf", [128, 128], "bfloat16")
-    SCRATCH["ta%d" % _b] = ("sbuf", [128, 256], "bfloat16")
-    SCRATCH["tb%d" % _b] = ("sbuf", [128, 512], "bfloat16")
-    SCRATCH["tg%d" % _b] = ("sbuf", [128, SL], "bfloat16")
-    SCRATCH["u%d" % _b] = ("sbuf", [128, UW], "float32")
-    for _k in range(4):
-        SCRATCH["ac%d%d" % (_b, _k)] = ("sbuf", [128, 256], "float32")
+    if _b % 2:
+        SCRATCH["ug%d" % _b] = ("sbuf", [128, F * NODES], "float32")
+        SCRATCH["us%d" % _b] = ("sbuf", [128, F * NODES], "float32")
+    else:
+        for _k in range(4):
+            SCRATCH["ac%d%d" % (_b, _k)] = ("sbuf", [128, 256], "float32")
     SCRATCH["yo%d" % _b] = ("sbuf", [128, 128], "float32")
 
 EVENTS = 144
@@ -57,6 +58,12 @@ def rank_program(g, core, T, topo):
     cores = list(T.cores)
     Q = {"g": g, "v": g.vector, "a": g.scalar, "s": g.sync, "t": g.tensor}
     V, S, Y, TE = g.vector, g.scalar, g.sync, g.tensor
+
+    pair = r - r % 2
+    far = N // 2 - pair
+    mate = pair + 1 - r % 2
+    STAGES = ((mate,), (far, far + 1))
+    OWN, PART, NEAR, FAR = CAP * r, CAP * mate, CAP * pair, CAP * far
 
     made, seen = [], set()
 
@@ -80,32 +87,25 @@ def rank_program(g, core, T, topo):
                 e["w"] = True
                 Q[q].wait_ge(e["s"], e["n"])
 
-    def share(s, q):
-        es = topo.engines(cores[s], cores[(s + q) % N])
-        return (es[1::2], es[0::2]) if q == 1 else (es[0::2], es[1::2])
-
-    def count(s, q):
-        return sum(len(es) for es in share(s, q))
-
     def send(src, dst, stage, arrived, left):
         for part in (0, 1):
             tr = []
-            for q in STAGES[stage]:
-                d = (r + q) % N
+            for i, d in enumerate(STAGES[stage]):
                 rid, pid, _ = topo.addr(cores[d])
-                a, b = CAP * q, CAP * (N - q)
+                es = topo.engines(cores[r], cores[d])[(part + i) % 2::2]
+                a, b = CAP * d, CAP * r
                 if part == 0:
                     f, t = T[src + "c"][:, a:a + CAP].bitcast(dt.uint8), T[dst + "c"][:, b:b + CAP].bitcast(dt.uint8)
                 else:
                     f, t = T[src + "p"][:, a:a + CAP], T[dst + "p"][:, b:b + CAP]
-                tr.append(RemoteDMATransfer(dst_ids=[DstId(rid=rid, pnc=pid)], dma_engine_mask=sum(1 << e for e in share(r, q)[part]),
+                tr.append(RemoteDMATransfer(dst_ids=[DstId(rid=rid, pnc=pid)], dma_engine_mask=sum(1 << e for e in es),
                                             remote_sem=arrived, src=f, dst=t))
             g.remote_dma_fused(tr, local_sem=left)
 
-    arrive = [sum(count((r - q) % N, q) for q in st) for st in STAGES]
-    sent = sum(count(r, q) for st in STAGES for q in st)
+    arrive = [sum(len(topo.engines(cores[s], cores[r])) for s in st) for st in STAGES]
+    sent = sum(len(topo.engines(cores[r], cores[d])) for st in STAGES for d in st)
 
-    e_x, e_sn, e_w, e_dnb, e_nb, e_gr = ev(), ev(), ev(), ev(), ev(), ev()
+    e_x, e_sn, e_w, e_dnb, e_nb, e_gr, e_inv, e_iln = ev(), ev(), ev(), ev(), ev(), ev(), ev(), ev()
     inc(Y.dma_start(T.xt[:, :], T.x[:, :]), e_x, 16)
     for p in range(4):
         inc(Y.dma_start(T.snl[16 * p:16 * p + 16, :], T.sn[:, :]), e_sn, 16)
@@ -114,29 +114,35 @@ def rank_program(g, core, T, topo):
     for i, k in enumerate(ORDER):
         inc(S.dma_start(T.dnb[:, 8 * i:8 * i + 8], T.nb[k:16:4, :]), e_dnb, 16)
     inc(S.dma_start(T.wt[:, :], T.w[:, :]), e_w, 16)
+    inc(Y.dma_start(T.grt[:, :], T.gr[:, :]), e_gr, 16)
+    inc(Y.dma_start(T.inv[0:1, :], T.sn[:, :]), e_inv, 16)
     need("s", e_dnb)
     for p in range(8):
         inc(Y.dma_start(T.nbl[16 * p:16 * p + 16, :], T.dnb[:, :]), e_nb, 16)
-    inc(Y.dma_start(T.grt[:, :], T.gr[:, :]), e_gr, 16)
+    for p in range(8):
+        inc(Y.dma_start(T.iln[16 * p:16 * p + 16, :], T.il[:, :]), e_iln, 16)
 
     e_p, e_zero, e_p12 = ev(), ev(), ev()
     inc(g.iota(T.pidx[:, 0:1], [[1, 1]], 0, 1), e_p)
     inc(g.iota(T.gio[:, :], [[1, 4], [16, 8]], 0, 0), e_p)
-    e_vals = do(g.iota(T.vals[:, :], [[1, 2], [256, 2], [2, NODES]], 0, 0))
-    inc(V.memset(T.inv[:, :], 0), e_zero)
+    e_vals = do(g.iota(T.vals[:, :], [[3 * NODES, 4], [3, NODES]], 2, 0))
+    inc(V.memset(T.d0[:, 0:4 * TR:3], 0.0), e_zero)
     need("v", e_p)
     inc(V.tensor_scalar(T.p12[:, 0:1], T.pidx[:, 0:1], 12, None, A.bitwise_and), e_p12)
     inc(V.tensor_scalar(T.p3[:, 0:1], T.pidx[:, 0:1], 3, None, A.bitwise_and), e_p12)
-    inc(V.memset(T.u0[:, SL:UW], 0.0), e_zero)
+    inc(V.memset(T.d1[:, 2:4 * TR:3], 0.0), e_zero)
     need("v", e_p12)
     e_p12f = do(V.tensor_copy(T.p12f[:, 0:1], T.p12[:, 0:1]))
-    inc(V.memset(T.u1[:, SL:UW], 0.0), e_zero)
+    for b in (0, 1):
+        inc(V.memset(T.d1[:, TR * b + 1:TR * b + TR // 2:3], 0.0), e_zero)
     need("v", e_p12f)
     e_ppf = do(V.tensor_scalar(T.ppf[:, 0:1], T.p3[:, 0:1], 128.0, T.p12f[:, 0:1], A.mult, A.add))
-    inc(V.memset(T.u2[:, SL:UW], 0.0), e_zero)
+    for b in (2, 3):
+        inc(V.memset(T.d1[:, TR * b + 1:TR * b + TR // 2:3], 0.0), e_zero)
     need("v", e_ppf)
     e_glo = do(V.tensor_scalar(T.glo[:, :], T.gio[:, :], T.ppf[:, 0:1], None, A.add))
-    inc(V.memset(T.u3[:, SL:UW], 0.0), e_zero)
+    inc(V.memset(T.uu[:, 0:4 * UW:UW], 0.0), e_zero)
+    inc(V.memset(T.mk[:, :], 0.0), e_zero)
 
     need("v", e_sn)
     e_so = [ev(), ev(), ev()]
@@ -144,256 +150,267 @@ def rank_program(g, core, T, topo):
     for t in range(4):
         inc(V.tensor_scalar(T["so%d" % t][:, :], T.snl[:, :], 4.0, float(t), A.mult, A.add), e_so[t])
 
-    def pick(q, t, runs, e):
-        pos, at = CAP * runs[0], [(r + i) % N for i in runs]
-        parts = [(at[0], len(at))] if at[-1] - at[0] == len(at) - 1 else [(d, 1) for d in at]
-        for d, n in parts:
-            out = T.xg[:, 4 * pos + t:4 * (pos + n * CAP):4]
-            win = T.xt[:, 0:512].indirect(T["so%d" % t][:, 10 * d:10 * (d + n)])
-            inc(S.activation(out, win, Act.Copy) if q == "a" else V.tensor_copy(out, win), e)
-            pos += n * CAP
+    def copy(q, out, src, e):
+        return inc(S.activation(out, src, Act.Copy) if q == "a" else V.tensor_copy(out, src), e)
 
-    def pack(dst, src, runs):
-        a, b = CAP * runs[0], CAP * (runs[-1] + 1)
+    def pick(q, t, at, e):
+        lo, hi = CAP * at[0], CAP * (at[-1] + 1)
+        copy(q, T.xg[:, 4 * lo + t:4 * hi:4], T.xt[:, 0:512].indirect(T["so%d" % t][:, lo // 16:hi // 16]), e)
+
+    def pack(dst, src, at):
+        a, b = CAP * at[0], CAP * (at[-1] + 1)
         return do(V.quantize_mx(T[dst + "c"][:, a:b], T[dst + "p"][:, a:b], T[src][:, 4 * a:4 * b]))
 
     need("a", e_x)
     need("v", e_x)
-    for stage, runs in enumerate(STAGES):
+    for stage, at in enumerate(STAGES):
         e_g = ev()
         for t in (0, 1):
             need("a", e_so[t])
-            pick("a", t, runs, e_g)
+            pick("a", t, at, e_g)
         for t in (2, 3):
             need("v", e_so[t])
-            pick("v", t, runs, e_g)
+            pick("v", t, at, e_g)
         need("v", e_g)
-        need("g", pack("sx", "xg", runs))
+        need("g", pack("sx", "xg", at))
         send("sx", "lx", stage, T.sem["ax%d" % stage], T.sem.sentx)
 
     e_xo = ev()
     for t in range(4):
         need("a", e_so[t])
-        pick("a", t, (0,), e_xo)
+        pick("a", t, (r,), e_xo)
     need("a", e_gr, e_glo)
-    e_grp = do(S.activation(T.grp[:, :], T.grt[:, 0:512].indirect(T.glo[:, 0:32]), Act.Copy))
-    need("v", e_w)
-    e_wq = do(V.quantize_mx(T.wqc[:, 0:512], T.wqp[:, 0:512], T.wt[:, 0:2048]))
+    e_grp = ev()
+    for b in range(4):
+        copy("a", T.d1[:, TR * b:TR * b + TR // 2:3], T.grt[:, 0:512].indirect(T.glo[:, 8 * b:8 * b + 8]), e_grp)
     need("v", e_nb)
-    rel = T.nbl
-    if r:
-        e = do(V.tensor_scalar(T.nb1[:, :], T.nbl[:, :], float(CAP * r), float(SL), A.is_lt, A.mult))
-        need("v", e)
-        e = do(V.tensor_tensor(T.nb2[:, :], T.nbl[:, :], T.nb1[:, :], A.add))
-        need("v", e)
-        e = do(V.tensor_scalar(T.nb3[:, :], T.nb2[:, :], float(-CAP * r), None, A.add))
-        need("v", e)
-        rel = T.nb3
-    e_4 = do(V.tensor_scalar(T.nb4[:, :], rel[:, :], 4, None, A.arith_shift_right))
-    e_nbo = do(V.tensor_copy(T.nbo[:, :], rel[:, :]))
-    e_56 = do(V.tensor_scalar(T.nb5[:, :], rel[:, :], 40.0, None, A.mult))
+    e_4 = do(V.tensor_scalar(T.nb4[:, :], T.nbl[:, :], 4, None, A.arith_shift_right))
+    e_nbo = do(V.tensor_copy(T.nbo[:, :], T.nbl[:, :]))
+    e_56 = do(V.tensor_scalar(T.nb5[:, :], T.nbl[:, :], 40.0, None, A.mult))
     need("v", e_4)
     inc(V.tensor_scalar(T.nb6[:, :], T.nb4[:, :], -639.0, None, A.mult), e_56)
     need("v", e_xo)
-    e_xoq = pack("lx", "xg", (0,))
+    e_xoq = pack("lx", "xg", (r,))
     need("v", e_56)
     e = do(V.tensor_tensor(T.nb7[:, :], T.nb5[:, :], T.nb6[:, :], A.add))
+    need("v", e_w)
+    e_wq = do(V.quantize_mx(T.wqc[:, 0:512], T.wqp[:, 0:512], T.wt[:, 0:2048]))
     need("v", e)
     e = do(V.tensor_copy(T.nbi[:, :], T.nb7[:, :]))
-    need("v", e, e_vals, e_zero)
+    need("v", e_zero)
+    e_mk = do(V.memset(T.mk[:, 2:TR:3], -1.0))
+    need("v", e, e_vals, e_inv)
     e_sc = do(V.tensor_copy(T.inv[:, 0:SL].indirect(T.nbi[:, 0:32]), T.vals[:, 0:512]))
+    need("v", e_grp)
+    e_d1 = {}
+    for b in range(4):
+        e_d1[b] = ev()
+        src = T.d1[:, TR * b:TR * b + TR // 2:3]
+        inc(V.tensor_copy(T.d1[:, TR * b + TR // 2 + 1:TR * b + TR:3], src), e_d1[b])
+        inc(V.tensor_scalar(T.d1[:, TR * b + TR // 2:TR * b + TR:3], src, -1.0, None, A.mult), e_d1[b])
     e_iv = ev()
     need("s", e_sc)
     for p in range(8):
-        inc(Y.dma_start(T.iv[16 * p:16 * p + 16, :], T.inv[16 * p:16 * p + 1, :]), e_iv, 16)
+        inc(Y.dma_start(T.iv[16 * p:16 * p + 16, :], T.inv[0:1, :]), e_iv, 16)
 
     e_dil, e_il, e_w2 = ev(), ev(), ev()
     g.wait_ge(T.sem.sentx, sent)
-    need("g", e_iv)
     for q in range(8):
         inc(g.dma_start(T.dil[2 * q:2 * q + 2, :], T.il[:, q:64:8], allow_slow_non_contiguous=True), e_dil, 16)
 
-    BANK = {(0, 0): 0, (0, 1): 1, (1, 0): 2, (2, 0): 3, (3, 0): 4}
-    FIRST = (5, 6, 7, 4)
     last = {}
 
-    def product(bank, st, b, mv, a, w):
-        if bank in last:
-            need("t", last[bank])
-        return do(TE.matmul_mx(T.ps[:, 512 * bank:512 * bank + w], T[st + "c"][:, 128 * b:128 * b + 128], T[st + "p"][:, 128 * b:128 * b + 128],
-                               T[mv + "c"][:, a:a + w], T[mv + "p"][:, a:a + w], True, True))
+    def products(st, mv, order, arrived):
+        out, met = {}, []
+        for b, late in order:
+            bank, a = (4 + b, FAR) if late else (b, NEAR)
+            if late and not met:
+                met.append(TE.wait_ge(arrived, arrive[1]))
+            if bank in last:
+                need("t", last[bank])
+            out[b, late] = do(TE.matmul_mx(T.ps[:, 512 * bank:512 * bank + HF], T[st + "c"][:, 128 * b:128 * b + 128], T[st + "p"][:, 128 * b:128 * b + 128],
+                                           T[mv + "c"][:, a:a + HF], T[mv + "p"][:, a:a + HF], True, True))
+        return out
 
-    def take(q, bank, w, out, e_mm):
-        need(q, e_mm)
-        src = T.ps[:, 512 * bank:512 * bank + w]
-        last[bank] = do(S.activation(out, src, Act.Copy) if q == "a" else V.tensor_copy(out, src))
+    def take(q, b, late, out, e_mm):
+        bank = 4 + b if late else b
+        need(q, e_mm[b, late])
+        last[bank] = copy(q, out, T.ps[:, 512 * bank:512 * bank + HF], ev())
         return last[bank]
 
-    def first(st, mv, to):
-        e = [product(FIRST[b], st, b, mv, 0, HF) for b in range(4)]
-        return {b: [take("a", FIRST[b], HF, T["%s%d" % (to, b)][:, 0:HF], e[b])] for b in range(4)}
+    def zpart(b, late):
+        a = FAR if late else NEAR
+        return T["z%d" % b][:, a:a + HF]
 
-    def second(st, mv):
-        return {bh: product(bank, st, bh[0], mv, HF + CAP * bh[1], CAP if bh[0] == 0 else HF) for bh, bank in BANK.items()}
+    def upart(b, late):
+        a = UW * b + 1 + (FAR if late else NEAR)
+        return T.uu[:, a:a + HF]
 
-    def rest(q, to, b, h, e_mm):
-        lo, w = HF + CAP * h, CAP if b == 0 else HF
-        return take(q, BANK[b, h], w, T["%s%d" % (to, b)][:, lo:lo + w], e_mm[b, h])
-
+    FIRST = ((0, 0), (1, 0), (0, 1), (1, 1), (2, 0), (2, 1), (3, 0), (3, 1))
     need("t", e_wq, e_xoq)
     TE.wait_ge(T.sem.ax0, arrive[0])
-    e_z = first("wq", "lx", "z")
-    TE.wait_ge(T.sem.ax1, arrive[1])
-    e_mz = second("wq", "lx")
-    need("s", e_mz[0, 0])
+    e_m = products("wq", "lx", FIRST, T.sem.ax1)
+    need("s", e_m[0, 1])
     inc(Y.dma_start(T.w2t[:, :], T.w2[:, :]), e_w2, 16)
     need("s", e_dil)
     for p in range(8):
         inc(Y.dma_start(T.ill[16 * p:16 * p + 16, :], T.dil[:, :]), e_il, 16)
 
-    e_zs, e_cc, e_mm, e_c, e_a, e_b, e_cm, e_t2, e_t2o = {}, {}, {}, {}, {}, {}, {}, {}, {}
+    e_z = {b: [] for b in range(4)}
+    e_zs, e_cc, e_mm, e_c, e_cp, e_ch, e_df = {}, {}, {}, {}, {}, {}, {}
 
     def zs(b):
         need("a", e_nbo, *e_z[b])
         e_zs[b] = do(S.activation(T["zs%d" % b][:, :], T["z%d" % b][:, 0:SL].indirect(T.nbo[:, 16:32]), Act.Copy))
 
-    def cc(b):
+    def pairs(b, out, op):
         need("v", e_nbo, e_zs[b], *e_z[b])
-        e_cc[b] = do(V.tensor_tensor(T["tb%d" % b][:, 0:512:2], T["z%d" % b][:, 0:SL].indirect(T.nbo[:, 0:16]), T["zs%d" % b][:, :], A.is_ge))
+        return do(V.tensor_tensor(out, T["z%d" % b][:, 0:SL].indirect(T.nbo[:, 0:16]), T["zs%d" % b][:, :], op))
+
+    def cc(b):
+        e_cc[b] = pairs(b, T.d0[:, TR * b + 2:TR * b + TR:3], A.is_ge)
 
     def mm(b):
-        e_mm[b] = do(V.tensor_tensor(T["mm%d" % b][:, :], T["z%d" % b][:, 0:SL].indirect(T.nbo[:, 0:16]), T["zs%d" % b][:, :], A.max))
+        e_mm[b] = pairs(b, T["mm%d" % b][:, :], A.max)
 
     def c(b):
         need("v", e_mm[b])
-        e_c[b] = do(V.tensor_tensor(T["cw%d" % b][:, :], T["mm%d" % b][:, 0:128], T["mm%d" % b][:, 128:256], A.is_ge))
+        e_c[b] = do(V.tensor_tensor(T.d0[:, TR * b + 1:TR * b + TR // 2:3], T["mm%d" % b][:, 0:128], T["mm%d" % b][:, 128:256], A.is_ge))
 
-    def ta(b):
-        need("v", e_c[b], e_grp)
-        e_a[b] = do(V.tensor_tensor(T["ta%d" % b][:, 0:128], T.grp[:, 128 * b:128 * b + 128], T["cw%d" % b][:, :], A.mult))
+    def cp(b):
+        need("v", e_c[b])
+        e_cp[b] = do(V.tensor_copy(T.d0[:, TR * b + TR // 2 + 1:TR * b + TR:3], T.d0[:, TR * b + 1:TR * b + TR // 2:3]))
 
-    def tb(b):
-        need("v", e_a[b])
-        e_b[b] = do(V.tensor_tensor(T["ta%d" % b][:, 128:256], T.grp[:, 128 * b:128 * b + 128], T["ta%d" % b][:, 0:128], A.subtract))
+    def ch(b):
+        need("v", e_zero, e_d1[b], e_cc[b], e_cp[b])
+        e_ch[b] = do(V.tensor_tensor_scan(T.gb[:, 2 * TR * b:2 * TR * b + TR], T.d0[:, TR * b:TR * b + TR], T.d1[:, TR * b:TR * b + TR], 0.0, A.mult, A.add))
 
-    def lists():
-        need("v", e_iv)
-        e_l = do(V.tensor_scalar(T.ivh[:, :], T.iv[:, :], 1, None, A.arith_shift_right))
-        e = do(V.tensor_copy(T.lt2[:, :], T.iv[:, :]))
-        need("v", e_l)
-        return inc(V.tensor_copy(T.lt1[:, :], T.ivh[:, :]), e)
+    def df(b):
+        need("v", e_mk, e_ch[b])
+        e_df[b] = do(V.tensor_tensor_scan(T.gb[:, 2 * TR * b + TR:2 * TR * b + 2 * TR], T.mk[:, :], T.gb[:, 2 * TR * b:2 * TR * b + TR], 0.0, A.mult, A.subtract))
 
-    def other(b):
-        need("a", e_cc[b])
-        e_cm[b] = do(S.activation(T["tb%d" % b][:, 1:512:2], T["tb%d" % b][:, 0:512:2], Act.Identity, bias=1.0, scale=-1.0))
+    def grad(q, b, lo, hi, e):
+        need(q, e_lt, e_ch[b], e_df[b])
+        copy(q, T.gt[:, 4 * lo + b:4 * hi:4], T.gb[:, 2 * TR * b:2 * TR * b + 2 * TR].indirect(T.lt[:, lo // 16:hi // 16]), e)
 
-    def t2(b, lo, hi, to):
-        need("a", e_cm[b], e_lt)
-        to[b] = do(S.activation(T["tg%d" % b][:, lo:hi], T["tb%d" % b][:, 0:512].indirect(T.lt2[:, lo // 16:hi // 16]), Act.Copy))
-
-    def grad(b, lo, hi, e):
-        need("v", e_lt, (e_t2 if lo else e_t2o)[b], e_a[b], e_b[b])
-        inc(V.tensor_tensor(T.gt[:, 4 * lo + b:4 * hi:4], T["ta%d" % b][:, 0:256].indirect(T.lt1[:, lo // 16:hi // 16]),
-                            T["tg%d" % b][:, lo:hi], A.mult), e)
-
-    e_z[0].append(rest("a", "z", 0, 0, e_mz))
-    e_z[0].append(rest("v", "z", 0, 1, e_mz))
-    zs(0)
-    for b in (1, 2, 3):
-        e_z[b].append(rest("a", "z", b, 0, e_mz))
-        zs(b)
+    for b, late in FIRST:
+        e_z[b].append(take("a", b, late, zpart(b, late), e_m))
+        if late:
+            zs(b)
     cc(0)
     mm(0)
     cc(1)
     c(0)
     mm(1)
-    ta(0)
+    cp(0)
     c(1)
-    tb(0)
+    ch(0)
+    cp(1)
+    need("v", e_iv)
+    e_lt = do(V.tensor_copy(T.lt[:, :], T.iv[:, :]))
+    df(0)
     cc(2)
-    ta(1)
-    e_lt = lists()
+    ch(1)
     mm(2)
-    tb(1)
-    c(2)
+    df(1)
     cc(3)
-    ta(2)
+    c(2)
     mm(3)
-    tb(2)
+    cp(2)
     c(3)
-    for b in range(4):
-        other(b)
-        t2(b, CAP, SL, e_t2)
-    B3 = 3 * CAP
-    e_g3, e_g12, e_g0 = ev(), ev(), ev()
-    grad(0, CAP, SL, e_g3)
-    ta(3)
-    grad(1, CAP, SL, e_g3)
-    tb(3)
-    grad(2, CAP, SL, e_g3)
-    grad(3, B3, SL, e_g3)
-    need("v", e_g3)
+    ch(2)
+    cp(3)
+    df(2)
+    ch(3)
+    df(3)
+    e_g0, e_g1, e_g2 = ev(), ev(), ev()
+    grad("a", 0, 0, SL, e_g0)
+    grad("a", 1, 0, SL, e_g0)
+    grad("a", 2, PART, PART + CAP, e_g0)
+    grad("a", 2, FAR, FAR + HF, e_g1)
+    grad("a", 3, FAR, FAR + HF, e_g1)
+    grad("v", 3, PART, PART + CAP, e_g0)
+    need("v", e_g0)
     need("g", pack("sg", "gt", STAGES[0]))
     send("sg", "lg", 0, T.sem.ag0, T.sem.sentg)
-    grad(3, CAP, B3, e_g12)
-    need("v", e_g12)
+    need("v", e_g1)
     need("g", pack("sg", "gt", STAGES[1]))
     send("sg", "lg", 1, T.sem.ag1, T.sem.sentg)
 
-    for b in range(4):
-        t2(b, 0, CAP, e_t2o)
-    for b in range(4):
-        grad(b, 0, CAP, e_g0)
+    for b in (2, 3):
+        grad("a", b, OWN, OWN + CAP, e_g2)
+    e = do(V.memset(T.rs[:, :], 1.0))
     need("v", e_w2)
     e_vq = do(V.quantize_mx(T.vqc[:, 0:512], T.vqp[:, 0:512], T.w2t[:, 0:2048]))
-    need("v", e_g0)
-    e_goq = pack("lg", "gt", (0,))
-    need("v", e_il)
-    e_i1 = do(V.tensor_scalar(T.il1[:, :], T.ill[:, :], float(CAP * r), float(SL), A.is_lt, A.mult))
-    e_i2 = do(V.tensor_scalar(T.il2[:, :], T.ill[:, :], 0.0, float(CAP * r + 1), A.is_lt, A.mult))
-    need("v", e_i1)
-    inc(V.tensor_tensor(T.il3[:, :], T.ill[:, :], T.il1[:, :], A.add), e_i2)
-    need("v", e_i2)
-    e = do(V.tensor_tensor(T.il4[:, :], T.il3[:, :], T.il2[:, :], A.add))
+    need("v", e_g2)
+    e_goq = pack("lg", "gt", (r,))
     need("v", e)
-    e_ilo = do(V.tensor_scalar(T.ilo[:, :], T.il4[:, :], float(-CAP * r), None, A.add))
+    e_rs = do(V.memset(T.rs[:, 0:F * NODES:F], 0.0))
+    need("v", e_il, e_iln)
+    e_ilo = do(V.tensor_scalar(T.ilo[:, :], T.ill[:, :], 1.0, None, A.add))
+    e_ilp = do(V.tensor_scalar(T.ilp[:, :], T.iln[:, :], 1.0, None, A.add))
 
     need("t", e_vq, e_goq)
     TE.wait_ge(T.sem.ag0, arrive[0])
-    e_u = first("vq", "lg", "u")
-    TE.wait_ge(T.sem.ag1, arrive[1])
-    e_mu = second("vq", "lg")
+    e_m = products("vq", "lg", ((0, 0), (2, 0), (1, 0), (0, 1), (2, 1), (1, 1), (3, 0), (3, 1)), T.sem.ag1)
 
-    e_ac = {}
+    e_u = {b: [] for b in range(4)}
+    e_ac, e_ug, e_us, e_y = {}, {}, {}, ev()
 
-    def us(b):
+    def win(b):
+        return T.uu[:, UW * b:UW * b + SL + 1]
+
+    def bring(q, b, late):
+        e_u[b].append(take(q, b, late, upart(b, late), e_m))
+
+    def places(b):
         need("a", e_ilo, e_zero, *e_u[b])
-        e_ac[b] = do(S.activation(T["ac%d0" % b][:, :], T["u%d" % b][:, 0:UW].indirect(T.ilo[:, 48:64]), Act.Copy))
+        e_ac[b] = do(S.activation(T["ac%d0" % b][:, :], win(b).indirect(T.ilo[:, 48:64]), Act.Copy))
+
+    def every(b):
+        need("a", e_ilp, e_zero, *e_u[b])
+        e_ug[b] = do(S.activation(T["ug%d" % b][:, :], win(b).indirect(T.ilp[:, 0:64]), Act.Copy))
 
     def add(b, i):
         need("v", e_ilo, e_ac[b], *e_u[b])
-        e_ac[b] = do(V.tensor_tensor(T["ac%d%d" % (b, i + 1)][:, :], T["u%d" % b][:, 0:UW].indirect(T.ilo[:, 16 * i:16 * i + 16]),
-                                     T["ac%d%d" % (b, i)][:, :], A.add))
+        e_ac[b] = do(V.tensor_tensor(T["ac%d%d" % (b, i + 1)][:, :], win(b).indirect(T.ilo[:, 16 * i:16 * i + 16]), T["ac%d%d" % (b, i)][:, :], A.add))
 
-    e_y = ev()
+    def scan(b):
+        need("v", e_rs, e_ug[b])
+        e_us[b] = do(V.tensor_tensor_scan(T["us%d" % b][:, :], T.rs[:, :], T["ug%d" % b][:, :], 0.0, A.mult, A.add))
 
-    def out(b):
-        need("v", e_ac[b])
-        e = do(V.tensor_tensor(T["yo%d" % b][:, :], T["ac%d3" % b][:, 0:128], T["ac%d3" % b][:, 128:256], A.add))
+    def out(q, b):
+        e = ev()
+        if b % 2:
+            need(q, e_us[b])
+            copy(q, T["yo%d" % b][:, :], T["us%d" % b][:, F - 1:F * NODES:F], e)
+        else:
+            need(q, e_ac[b])
+            inc(V.tensor_tensor(T["yo%d" % b][:, :], T["ac%d3" % b][:, 0:128], T["ac%d3" % b][:, 128:256], A.add), e)
         need("s", e)
         inc(Y.dma_start(T.y[:, 128 * b:128 * b + 128], T["yo%d" % b][:, :]), e_y, 16)
 
-    e_u[0].append(rest("a", "u", 0, 0, e_mu))
-    e_u[0].append(rest("v", "u", 0, 1, e_mu))
-    us(0)
-    for b in (1, 2, 3):
-        e_u[b].append(rest("a", "u", b, 0, e_mu))
-        us(b)
-    for b, i in ((0, 0), (0, 1), (1, 0), (0, 2), (1, 1), (0, 3), (1, 2), (2, 0), (1, 3), (2, 1), (3, 0), (2, 2), (3, 1), (2, 3), (3, 2), (3, 3)):
-        if i < 3:
-            add(b, i)
-        else:
-            out(b)
+    bring("a", 0, 0)
+    bring("v", 2, 0)
+    bring("v", 1, 0)
+    bring("a", 0, 1)
+    bring("v", 2, 1)
+    places(0)
+    bring("v", 1, 1)
+    places(2)
+    every(1)
+    bring("a", 3, 0)
+    bring("a", 3, 1)
+    every(3)
+    for i in range(3):
+        add(0, i)
+        add(2, i)
+    out("v", 0)
+    scan(1)
+    out("v", 2)
+    scan(3)
+    out("a", 1)
+    out("v", 3)
     need("s", e_y)
     g.wait_ge(T.sem.sentg, sent)
     for e in made:

import numpy as np
from concourse.bass import DstId, RemoteDMATransfer
from concourse.mybir import dt, AluOpType, ActivationFunctionType

N, NODES, CAP, F = 4, 128, 160, 8
SL = N * CAP
HF = 2 * CAP
UW = SL + 8
TR = 3 * 2 * NODES
ORDER = (0, 2, 1, 3)

SCRATCH = {
    "snl": ("sbuf", [128, SL // 16], "int32"), "nbl": ("sbuf", [128, 32], "int32"), "dnb": ("dram", [16, 32], "int32"),
    "nbo": ("sbuf", [128, 32], "uint16"), "nbi": ("sbuf", [128, 32], "uint16"),
    "ill": ("sbuf", [128, 64], "int32"), "ilo": ("sbuf", [128, 64], "uint16"), "dil": ("dram", [16, 64], "int32"),
    "iln": ("sbuf", [128, 64], "int32"), "ilp": ("sbuf", [128, 64], "uint16"),
    "glo": ("sbuf", [128, 32], "uint16"), "gio": ("sbuf", [128, 32], "int32"),
    "pidx": ("sbuf", [128, 1], "int32"), "p12": ("sbuf", [128, 1], "int32"), "p3": ("sbuf", [128, 1], "int32"),
    "p12f": ("sbuf", [128, 1], "float32"), "ppf": ("sbuf", [128, 1], "float32"),
    "vals": ("sbuf", [128, 512], "int32"), "inv": ("sbuf", [128, SL], "int32"),
    "iv": ("sbuf", [128, 40], "int32"), "lt": ("sbuf", [128, 40], "uint16"),
    "xt": ("sbuf", [128, 512], "bfloat16"), "grt": ("sbuf", [128, 512], "bfloat16"),
    "wt": ("sbuf", [128, 2048], "bfloat16"), "w2t": ("sbuf", [128, 2048], "bfloat16"),
    "xg": ("sbuf", [128, 4 * SL], "bfloat16"), "gt": ("sbuf", [128, 4 * SL], "bfloat16"),
    "d0": ("sbuf", [128, 4 * TR], "bfloat16"), "d1": ("sbuf", [128, 4 * TR], "bfloat16"),
    "mk": ("sbuf", [128, TR], "bfloat16"), "gb": ("sbuf", [128, 8 * TR], "bfloat16"),
    "rs": ("sbuf", [128, F * NODES], "float32"),
    "uu": ("sbuf", [128, 4 * UW], "float32"),
    "ps": ("psum", [128, 4096], "float32"),
}
for _i in range(4, 8):
    SCRATCH["nb%d" % _i] = ("sbuf", [128, 32], "int32")
for _n, _w in (("wq", 512), ("vq", 512), ("sx", SL), ("sg", SL), ("lx", SL), ("lg", SL)):
    SCRATCH[_n + "c"] = ("sbuf", [128, _w], "float8_e4m3fn_x4")
    SCRATCH[_n + "p"] = ("sbuf", [128, _w], "uint8")
for _b in range(4):
    SCRATCH["so%d" % _b] = ("sbuf", [128, SL // 16], "uint16")
    SCRATCH["z%d" % _b] = ("sbuf", [128, SL], "float32")
    SCRATCH["zs%d" % _b] = ("sbuf", [128, 256], "float32")
    SCRATCH["mm%d" % _b] = ("sbuf", [128, 256], "float32")
    if _b % 2:
        SCRATCH["ug%d" % _b] = ("sbuf", [128, F * NODES], "float32")
        SCRATCH["us%d" % _b] = ("sbuf", [128, F * NODES], "float32")
    else:
        for _k in range(4):
            SCRATCH["ac%d%d" % (_b, _k)] = ("sbuf", [128, 256], "float32")
    SCRATCH["yo%d" % _b] = ("sbuf", [128, 128], "float32")

EVENTS = 144
SEMAPHORES = ["ax0", "ax1", "ag0", "ag1", "sentx", "sentg"] + ["e%d" % _i for _i in range(EVENTS)]


def rank_program(g, core, T, topo):
    r = T.rank_of(core)
    if r is None:
        return
    A, Act = AluOpType, ActivationFunctionType
    cores = list(T.cores)
    Q = {"g": g, "v": g.vector, "a": g.scalar, "s": g.sync, "t": g.tensor}
    V, S, Y, TE = g.vector, g.scalar, g.sync, g.tensor

    pair = r - r % 2
    far = N // 2 - pair
    mate = pair + 1 - r % 2
    STAGES = ((mate,), (far, far + 1))
    OWN, PART, NEAR, FAR = CAP * r, CAP * mate, CAP * pair, CAP * far

    made, seen = [], set()

    def ev():
        e = {"k": len(made), "s": T.sem["e%d" % len(made)], "n": 0, "w": False}
        made.append(e)
        return e

    def inc(op, e, n=1):
        op.then_inc(e["s"], n)
        e["n"] += n
        return e

    def do(op):
        return inc(op, ev())

    def need(q, *es):
        for e in es:
            if (q, e["k"]) not in seen:
                seen.add((q, e["k"]))
                e["w"] = True
                Q[q].wait_ge(e["s"], e["n"])

    def send(src, dst, stage, arrived, left):
        for part in (0, 1):
            tr = []
            for i, d in enumerate(STAGES[stage]):
                rid, pid, _ = topo.addr(cores[d])
                es = topo.engines(cores[r], cores[d])[(part + i) % 2::2]
                a, b = CAP * d, CAP * r
                if part == 0:
                    f, t = T[src + "c"][:, a:a + CAP].bitcast(dt.uint8), T[dst + "c"][:, b:b + CAP].bitcast(dt.uint8)
                else:
                    f, t = T[src + "p"][:, a:a + CAP], T[dst + "p"][:, b:b + CAP]
                tr.append(RemoteDMATransfer(dst_ids=[DstId(rid=rid, pnc=pid)], dma_engine_mask=sum(1 << e for e in es),
                                            remote_sem=arrived, src=f, dst=t))
            g.remote_dma_fused(tr, local_sem=left)

    arrive = [sum(len(topo.engines(cores[s], cores[r])) for s in st) for st in STAGES]
    sent = sum(len(topo.engines(cores[r], cores[d])) for st in STAGES for d in st)

    e_x, e_sn, e_w, e_dnb, e_nb, e_gr, e_inv, e_iln = ev(), ev(), ev(), ev(), ev(), ev(), ev(), ev()
    inc(Y.dma_start(T.xt[:, :], T.x[:, :]), e_x, 16)
    for p in range(4):
        inc(Y.dma_start(T.snl[16 * p:16 * p + 16, :], T.sn[:, :]), e_sn, 16)
    for p in range(4, 8):
        inc(S.dma_start(T.snl[16 * p:16 * p + 16, :], T.sn[:, :]), e_sn, 16)
    for i, k in enumerate(ORDER):
        inc(S.dma_start(T.dnb[:, 8 * i:8 * i + 8], T.nb[k:16:4, :]), e_dnb, 16)
    inc(S.dma_start(T.wt[:, :], T.w[:, :]), e_w, 16)
    inc(Y.dma_start(T.grt[:, :], T.gr[:, :]), e_gr, 16)
    inc(Y.dma_start(T.inv[0:1, :], T.sn[:, :]), e_inv, 16)
    need("s", e_dnb)
    for p in range(8):
        inc(Y.dma_start(T.nbl[16 * p:16 * p + 16, :], T.dnb[:, :]), e_nb, 16)
    for p in range(8):
        inc(Y.dma_start(T.iln[16 * p:16 * p + 16, :], T.il[:, :]), e_iln, 16)

    e_p, e_zero, e_p12 = ev(), ev(), ev()
    inc(g.iota(T.pidx[:, 0:1], [[1, 1]], 0, 1), e_p)
    inc(g.iota(T.gio[:, :], [[1, 4], [16, 8]], 0, 0), e_p)
    e_vals = do(g.iota(T.vals[:, :], [[3 * NODES, 4], [3, NODES]], 2, 0))
    inc(V.memset(T.d0[:, 0:4 * TR:3], 0.0), e_zero)
    need("v", e_p)
    inc(V.tensor_scalar(T.p12[:, 0:1], T.pidx[:, 0:1], 12, None, A.bitwise_and), e_p12)
    inc(V.tensor_scalar(T.p3[:, 0:1], T.pidx[:, 0:1], 3, None, A.bitwise_and), e_p12)
    inc(V.memset(T.d1[:, 2:4 * TR:3], 0.0), e_zero)
    need("v", e_p12)
    e_p12f = do(V.tensor_copy(T.p12f[:, 0:1], T.p12[:, 0:1]))
    for b in (0, 1):
        inc(V.memset(T.d1[:, TR * b + 1:TR * b + TR // 2:3], 0.0), e_zero)
    need("v", e_p12f)
    e_ppf = do(V.tensor_scalar(T.ppf[:, 0:1], T.p3[:, 0:1], 128.0, T.p12f[:, 0:1], A.mult, A.add))
    for b in (2, 3):
        inc(V.memset(T.d1[:, TR * b + 1:TR * b + TR // 2:3], 0.0), e_zero)
    need("v", e_ppf)
    e_glo = do(V.tensor_scalar(T.glo[:, :], T.gio[:, :], T.ppf[:, 0:1], None, A.add))
    inc(V.memset(T.uu[:, 0:4 * UW:UW], 0.0), e_zero)
    inc(V.memset(T.mk[:, :], 0.0), e_zero)

    need("v", e_sn)
    e_so = [ev(), ev(), ev()]
    e_so.append(e_so[2])
    for t in range(4):
        inc(V.tensor_scalar(T["so%d" % t][:, :], T.snl[:, :], 4.0, float(t), A.mult, A.add), e_so[t])

    def copy(q, out, src, e):
        return inc(S.activation(out, src, Act.Copy) if q == "a" else V.tensor_copy(out, src), e)

    def pick(q, t, at, e):
        lo, hi = CAP * at[0], CAP * (at[-1] + 1)
        copy(q, T.xg[:, 4 * lo + t:4 * hi:4], T.xt[:, 0:512].indirect(T["so%d" % t][:, lo // 16:hi // 16]), e)

    def pack(dst, src, at):
        a, b = CAP * at[0], CAP * (at[-1] + 1)
        return do(V.quantize_mx(T[dst + "c"][:, a:b], T[dst + "p"][:, a:b], T[src][:, 4 * a:4 * b]))

    need("a", e_x)
    need("v", e_x)
    for stage, at in enumerate(STAGES):
        e_g = ev()
        for t in (0, 1):
            need("a", e_so[t])
            pick("a", t, at, e_g)
        for t in (2, 3):
            need("v", e_so[t])
            pick("v", t, at, e_g)
        need("v", e_g)
        need("g", pack("sx", "xg", at))
        send("sx", "lx", stage, T.sem["ax%d" % stage], T.sem.sentx)

    e_xo = ev()
    for t in range(4):
        need("a", e_so[t])
        pick("a", t, (r,), e_xo)
    need("a", e_gr, e_glo)
    e_grp = ev()
    for b in range(4):
        copy("a", T.d1[:, TR * b:TR * b + TR // 2:3], T.grt[:, 0:512].indirect(T.glo[:, 8 * b:8 * b + 8]), e_grp)
    need("v", e_nb)
    e_4 = do(V.tensor_scalar(T.nb4[:, :], T.nbl[:, :], 4, None, A.arith_shift_right))
    e_nbo = do(V.tensor_copy(T.nbo[:, :], T.nbl[:, :]))
    e_56 = do(V.tensor_scalar(T.nb5[:, :], T.nbl[:, :], 40.0, None, A.mult))
    need("v", e_4)
    inc(V.tensor_scalar(T.nb6[:, :], T.nb4[:, :], -639.0, None, A.mult), e_56)
    need("v", e_xo)
    e_xoq = pack("lx", "xg", (r,))
    need("v", e_56)
    e = do(V.tensor_tensor(T.nb7[:, :], T.nb5[:, :], T.nb6[:, :], A.add))
    need("v", e_w)
    e_wq = do(V.quantize_mx(T.wqc[:, 0:512], T.wqp[:, 0:512], T.wt[:, 0:2048]))
    need("v", e)
    e = do(V.tensor_copy(T.nbi[:, :], T.nb7[:, :]))
    need("v", e_zero)
    e_mk = do(V.memset(T.mk[:, 2:TR:3], -1.0))
    need("v", e, e_vals, e_inv)
    e_sc = do(V.tensor_copy(T.inv[:, 0:SL].indirect(T.nbi[:, 0:32]), T.vals[:, 0:512]))
    need("v", e_grp)
    e_d1 = {}
    for b in range(4):
        e_d1[b] = ev()
        src = T.d1[:, TR * b:TR * b + TR // 2:3]
        inc(V.tensor_copy(T.d1[:, TR * b + TR // 2 + 1:TR * b + TR:3], src), e_d1[b])
        inc(V.tensor_scalar(T.d1[:, TR * b + TR // 2:TR * b + TR:3], src, -1.0, None, A.mult), e_d1[b])
    e_iv = ev()
    need("s", e_sc)
    for p in range(8):
        inc(Y.dma_start(T.iv[16 * p:16 * p + 16, :], T.inv[0:1, :]), e_iv, 16)

    e_dil, e_il, e_w2 = ev(), ev(), ev()
    g.wait_ge(T.sem.sentx, sent)
    for q in range(8):
        inc(g.dma_start(T.dil[2 * q:2 * q + 2, :], T.il[:, q:64:8], allow_slow_non_contiguous=True), e_dil, 16)

    last = {}

    def products(st, mv, order, arrived):
        out, met = {}, []
        for b, late in order:
            bank, a = (4 + b, FAR) if late else (b, NEAR)
            if late and not met:
                met.append(TE.wait_ge(arrived, arrive[1]))
            if bank in last:
                need("t", last[bank])
            out[b, late] = do(TE.matmul_mx(T.ps[:, 512 * bank:512 * bank + HF], T[st + "c"][:, 128 * b:128 * b + 128], T[st + "p"][:, 128 * b:128 * b + 128],
                                           T[mv + "c"][:, a:a + HF], T[mv + "p"][:, a:a + HF], True, True))
        return out

    def take(q, b, late, out, e_mm):
        bank = 4 + b if late else b
        need(q, e_mm[b, late])
        last[bank] = copy(q, out, T.ps[:, 512 * bank:512 * bank + HF], ev())
        return last[bank]

    def zpart(b, late):
        a = FAR if late else NEAR
        return T["z%d" % b][:, a:a + HF]

    def upart(b, late):
        a = UW * b + 1 + (FAR if late else NEAR)
        return T.uu[:, a:a + HF]

    FIRST = ((0, 0), (1, 0), (0, 1), (1, 1), (2, 0), (2, 1), (3, 0), (3, 1))
    need("t", e_wq, e_xoq)
    TE.wait_ge(T.sem.ax0, arrive[0])
    e_m = products("wq", "lx", FIRST, T.sem.ax1)
    need("s", e_m[0, 1])
    inc(Y.dma_start(T.w2t[:, :], T.w2[:, :]), e_w2, 16)
    need("s", e_dil)
    for p in range(8):
        inc(Y.dma_start(T.ill[16 * p:16 * p + 16, :], T.dil[:, :]), e_il, 16)

    e_z = {b: [] for b in range(4)}
    e_zs, e_cc, e_mm, e_c, e_cp, e_ch, e_df = {}, {}, {}, {}, {}, {}, {}

    def zs(b):
        need("a", e_nbo, *e_z[b])
        e_zs[b] = do(S.activation(T["zs%d" % b][:, :], T["z%d" % b][:, 0:SL].indirect(T.nbo[:, 16:32]), Act.Copy))

    def pairs(b, out, op):
        need("v", e_nbo, e_zs[b], *e_z[b])
        return do(V.tensor_tensor(out, T["z%d" % b][:, 0:SL].indirect(T.nbo[:, 0:16]), T["zs%d" % b][:, :], op))

    def cc(b):
        e_cc[b] = pairs(b, T.d0[:, TR * b + 2:TR * b + TR:3], A.is_ge)

    def mm(b):
        e_mm[b] = pairs(b, T["mm%d" % b][:, :], A.max)

    def c(b):
        need("v", e_mm[b])
        e_c[b] = do(V.tensor_tensor(T.d0[:, TR * b + 1:TR * b + TR // 2:3], T["mm%d" % b][:, 0:128], T["mm%d" % b][:, 128:256], A.is_ge))

    def cp(b):
        need("v", e_c[b])
        e_cp[b] = do(V.tensor_copy(T.d0[:, TR * b + TR // 2 + 1:TR * b + TR:3], T.d0[:, TR * b + 1:TR * b + TR // 2:3]))

    def ch(b):
        need("v", e_zero, e_d1[b], e_cc[b], e_cp[b])
        e_ch[b] = do(V.tensor_tensor_scan(T.gb[:, 2 * TR * b:2 * TR * b + TR], T.d0[:, TR * b:TR * b + TR], T.d1[:, TR * b:TR * b + TR], 0.0, A.mult, A.add))

    def df(b):
        need("v", e_mk, e_ch[b])
        e_df[b] = do(V.tensor_tensor_scan(T.gb[:, 2 * TR * b + TR:2 * TR * b + 2 * TR], T.mk[:, :], T.gb[:, 2 * TR * b:2 * TR * b + TR], 0.0, A.mult, A.subtract))

    def grad(q, b, lo, hi, e):
        need(q, e_lt, e_ch[b], e_df[b])
        copy(q, T.gt[:, 4 * lo + b:4 * hi:4], T.gb[:, 2 * TR * b:2 * TR * b + 2 * TR].indirect(T.lt[:, lo // 16:hi // 16]), e)

    for b, late in FIRST:
        e_z[b].append(take("a", b, late, zpart(b, late), e_m))
        if late:
            zs(b)
    cc(0)
    mm(0)
    cc(1)
    c(0)
    mm(1)
    cp(0)
    c(1)
    ch(0)
    cp(1)
    need("v", e_iv)
    e_lt = do(V.tensor_copy(T.lt[:, :], T.iv[:, :]))
    df(0)
    cc(2)
    ch(1)
    mm(2)
    df(1)
    cc(3)
    c(2)
    mm(3)
    cp(2)
    c(3)
    ch(2)
    cp(3)
    df(2)
    ch(3)
    df(3)
    e_g0, e_g1, e_g2 = ev(), ev(), ev()
    grad("a", 0, 0, SL, e_g0)
    grad("a", 1, 0, SL, e_g0)
    grad("a", 2, PART, PART + CAP, e_g0)
    grad("a", 2, FAR, FAR + HF, e_g1)
    grad("a", 3, FAR, FAR + HF, e_g1)
    grad("v", 3, PART, PART + CAP, e_g0)
    need("v", e_g0)
    need("g", pack("sg", "gt", STAGES[0]))
    send("sg", "lg", 0, T.sem.ag0, T.sem.sentg)
    need("v", e_g1)
    need("g", pack("sg", "gt", STAGES[1]))
    send("sg", "lg", 1, T.sem.ag1, T.sem.sentg)

    for b in (2, 3):
        grad("a", b, OWN, OWN + CAP, e_g2)
    e = do(V.memset(T.rs[:, :], 1.0))
    need("v", e_w2)
    e_vq = do(V.quantize_mx(T.vqc[:, 0:512], T.vqp[:, 0:512], T.w2t[:, 0:2048]))
    need("v", e_g2)
    e_goq = pack("lg", "gt", (r,))
    need("v", e)
    e_rs = do(V.memset(T.rs[:, 0:F * NODES:F], 0.0))
    need("v", e_il, e_iln)
    e_ilo = do(V.tensor_scalar(T.ilo[:, :], T.ill[:, :], 1.0, None, A.add))
    e_ilp = do(V.tensor_scalar(T.ilp[:, :], T.iln[:, :], 1.0, None, A.add))

    need("t", e_vq, e_goq)
    TE.wait_ge(T.sem.ag0, arrive[0])
    e_m = products("vq", "lg", ((0, 0), (2, 0), (1, 0), (0, 1), (2, 1), (1, 1), (3, 0), (3, 1)), T.sem.ag1)

    e_u = {b: [] for b in range(4)}
    e_ac, e_ug, e_us, e_y = {}, {}, {}, ev()

    def win(b):
        return T.uu[:, UW * b:UW * b + SL + 1]

    def bring(q, b, late):
        e_u[b].append(take(q, b, late, upart(b, late), e_m))

    def places(b):
        need("a", e_ilo, e_zero, *e_u[b])
        e_ac[b] = do(S.activation(T["ac%d0" % b][:, :], win(b).indirect(T.ilo[:, 48:64]), Act.Copy))

    def every(b):
        need("a", e_ilp, e_zero, *e_u[b])
        e_ug[b] = do(S.activation(T["ug%d" % b][:, :], win(b).indirect(T.ilp[:, 0:64]), Act.Copy))

    def add(b, i):
        need("v", e_ilo, e_ac[b], *e_u[b])
        e_ac[b] = do(V.tensor_tensor(T["ac%d%d" % (b, i + 1)][:, :], win(b).indirect(T.ilo[:, 16 * i:16 * i + 16]), T["ac%d%d" % (b, i)][:, :], A.add))

    def scan(b):
        need("v", e_rs, e_ug[b])
        e_us[b] = do(V.tensor_tensor_scan(T["us%d" % b][:, :], T.rs[:, :], T["ug%d" % b][:, :], 0.0, A.mult, A.add))

    def out(q, b):
        e = ev()
        if b % 2:
            need(q, e_us[b])
            copy(q, T["yo%d" % b][:, :], T["us%d" % b][:, F - 1:F * NODES:F], e)
        else:
            need(q, e_ac[b])
            inc(V.tensor_tensor(T["yo%d" % b][:, :], T["ac%d3" % b][:, 0:128], T["ac%d3" % b][:, 128:256], A.add), e)
        need("s", e)
        inc(Y.dma_start(T.y[:, 128 * b:128 * b + 128], T["yo%d" % b][:, :]), e_y, 16)

    bring("a", 0, 0)
    bring("v", 2, 0)
    bring("v", 1, 0)
    bring("a", 0, 1)
    bring("v", 2, 1)
    places(0)
    bring("v", 1, 1)
    places(2)
    every(1)
    bring("a", 3, 0)
    bring("a", 3, 1)
    every(3)
    for i in range(3):
        add(0, i)
        add(2, i)
    out("v", 0)
    scan(1)
    out("v", 2)
    scan(3)
    out("a", 1)
    out("v", 3)
    need("s", e_y)
    g.wait_ge(T.sem.sentg, sent)
    for e in made:
        if not e["w"]:
            need("g", e)
